import numpy as np
import ml_dtypes


def mxq(x, axis, fmt="e4m3"):
    dtype, down = {"e4m3": (ml_dtypes.float8_e4m3fn, 7), "e5m2": (ml_dtypes.float8_e5m2, 14)}[fmt]
    v = np.moveaxis(np.asarray(x, np.float32).astype(ml_dtypes.bfloat16).astype(np.float64), axis, -1)
    blocks = v.reshape(v.shape[:-1] + (-1, 32))
    amax = np.abs(blocks).max(-1, keepdims=True)
    byte = np.maximum(np.where(amax > 0, np.frexp(amax)[1] - 1 + 127, 0) - down, 1)
    scale = np.exp2(byte - 127.0)
    codes = (blocks / scale).astype(np.float32).astype(dtype).astype(np.float64)
    return np.moveaxis((codes * scale).reshape(v.shape), -1, axis)


WIDE = False


def mx_kscale(k):
    if not WIDE:
        return np.ones(k)
    levels = np.array([10, -10, 5, -5, 0])
    if k % 512:
        return np.exp2(np.random.permutation(np.resize(levels, k // 32))).repeat(32)
    a = np.empty((k // 512, 16))
    for p in range(k // 512):
        a[p, :8] = np.random.permutation(np.resize(levels, 8))
        for g in range(8):
            far = levels[np.abs(levels - a[p, g]) >= 10]
            a[p, g + 8] = far[np.random.randint(len(far))]
    return np.exp2(a.ravel()).repeat(32)


BF16 = ml_dtypes.bfloat16


def bf(x):
    return np.asarray(x, np.float32).astype(BF16)


def f64(x):
    return np.asarray(x).astype(np.float64)


E2M1 = np.array([0.0, 0.5, 1.0, 1.5, 2.0, 3.0, 4.0, 6.0, -0.0, -0.5, -1.0, -1.5, -2.0, -3.0, -4.0, -6.0])


def pack_weight(w, fmt):
    k, n = w.shape
    w = f64(bf(w)).reshape(k // 32, 32, n)
    amax = np.abs(w).max(1)
    if fmt == "e4m3":
        byte = np.frexp(amax)[1] - 1 + 127 - 7
    else:
        mant, ex = np.frexp(amax / 6.0)
        byte = np.where(mant > 0.5, ex, ex - 1) + 127
    byte = np.clip(np.where(amax > 0, byte, 1), 1, 254)
    scaled = (w * np.exp2(127.0 - byte)[:, None, :]).reshape(k, n).astype(np.float32)
    by_word = np.ascontiguousarray(scaled.reshape(k // 512, 128, 4, n).transpose(0, 1, 3, 2))
    if fmt == "e4m3":
        words = by_word.astype(ml_dtypes.float8_e4m3fn).view(np.uint8)
    else:
        c = by_word.astype(ml_dtypes.float4_e2m1fn).view(np.uint8) & 0xF
        words = c[..., 0::2] | (c[..., 1::2] << 4)
    return np.ascontiguousarray(words), np.ascontiguousarray(byte.astype(np.uint8).reshape(k // 512, 16, n))


def unpack_weight(words, scales, fmt):
    g, p, n, _ = words.shape
    if fmt == "e4m3":
        vals = np.ascontiguousarray(words).view(ml_dtypes.float8_e4m3fn).astype(np.float64)
    else:
        nib = np.empty((g, p, n, 4), np.uint8)
        nib[..., 0::2] = words & 0xF
        nib[..., 1::2] = words >> 4
        vals = E2M1[nib]
    vals = vals * np.repeat(np.exp2(scales.astype(np.float64) - 127.0), 8, axis=1)[..., None]
    return vals.transpose(0, 1, 3, 2).reshape(g * 512, n)
def pack4(w):
    words, scales = pack_weight(w, "e2m1")
    return words.reshape(words.shape[0], 128, -1), scales


def unpack4(words, scales):
    return unpack_weight(words.reshape(words.shape[0], 128, -1, 2), scales, "e2m1")


M, K, N = 1536, 512, 1024


def draw0():
    s, u, t = mx_kscale(K), mx_kscale(M), mx_kscale(N)
    left = bf(np.random.standard_normal((M, K)) * s * u[:, None])
    right = bf(np.random.standard_normal((K, N)) / np.sqrt(K) / s[:, None])
    a = bf(np.random.standard_normal((M, M)) / np.sqrt(M) / u)
    d = bf((0.5 + np.random.random((M, N))) * t / u[:, None])
    b_words, b_scales = pack4(np.random.standard_normal((N, N)) / np.sqrt(N) / t[:, None])
    c = bf(np.random.standard_normal((M, N)))
    return {"left": left, "right": right, "a": a, "d": d,
            "b_words": b_words, "b_scales": b_scales, "c": c}


def core(left, right, a, d, b_words, b_scales, c):
    x = mxq(f64(left), 1, "e4m3") @ mxq(f64(right), 0, "e4m3")
    y = x * f64(d)
    ax = mxq(f64(a), 1, "e4m3") @ mxq(x, 0, "e4m3")
    yb = mxq(y, 1, "e4m3") @ unpack4(b_words, b_scales)
    return ax + yb - f64(c)


def e4m3fn_bytes(y):
    return np.clip(np.asarray(y, np.float64), -448.0, 448.0).astype(np.float32).astype(ml_dtypes.float8_e4m3fn).view(np.uint8)


def e4m3fn_values(b):
    return np.asarray(b, np.uint8).view(ml_dtypes.float8_e4m3fn).astype(np.float64)


def setup_inputs():
    d = draw0()
    x0 = np.asarray(d['a']).astype(np.float64)
    s = (np.max(np.abs(x0), axis=(0,), keepdims=True) / 448.0).astype(np.float32)
    out = {}
    for k, v in d.items():
        if k == 'a':
            out['a_bytes'] = e4m3fn_bytes(x0 / s.astype(np.float64))
            out['a_scale'] = s
        else:
            out[k] = v
    return out


def reference(left, right, a_bytes, a_scale, d, b_words, b_scales, c):
    return core(left, right, e4m3fn_values(a_bytes) * a_scale.astype(np.float64), d, b_words, b_scales, c)

@@ -1,0 +1,449 @@
+from contextlib import ExitStack
+
+import concourse.mybir as mybir
+from concourse.masks import make_identity
+
+M, K, N = 1536, 512, 1024
+FLOPS = 2 * M * K * N + 2 * M * M * N + 2 * M * N * N
+
+F32 = mybir.dt.float32
+BF16 = mybir.dt.bfloat16
+U32 = mybir.dt.uint32
+I32 = mybir.dt.int32
+U8 = mybir.dt.uint8
+FP8 = mybir.dt.float8_e4m3fn
+FP8X4 = mybir.dt.float8_e4m3fn_x4
+FP4X4 = mybir.dt.float4_e2m1fn_x4
+MULT = mybir.AluOpType.mult
+SUB = mybir.AluOpType.subtract
+
+P = 128
+GROUPS = M // 512
+HALVES = N // 512
+TURN_BANKS = (6, 7, 0, 1)
+ACC_BANKS = (4, 5, 2, 3)
+TILES = M // P
+
+
+def tile_sylvester_scaled_residual_s8_kernel(
+    tc, left, right, a_bytes, a_scale, d, b_words, b_scales, c, out
+):
+    nc = tc.nc
+    with ExitStack() as ctx:
+        keep = ctx.enter_context(tc.tile_pool(name="keep", bufs=1))
+        work = ctx.enter_context(tc.tile_pool(name="work", bufs=2))
+        psum = ctx.enter_context(tc.psum_pool(name="psum", bufs=1))
+
+        ident = keep.tile([P, P], F32, name="ident", align_bytes=64)
+        left_codes = keep.tile([P, M], U32, name="left_codes", align_bytes=64)
+        left_scales = keep.tile([P, M], U8, name="left_scales", align_bytes=64)
+        right_codes = keep.tile([P, N], U32, name="right_codes", align_bytes=64)
+        right_scales = keep.tile([P, N], U8, name="right_scales", align_bytes=64)
+        x_codes = keep.tile([P, GROUPS, N], U32, name="x_codes", align_bytes=64)
+        x_scales = keep.tile([P, GROUPS, N], U8, name="x_scales", align_bytes=64)
+        y_codes = keep.tile([P, HALVES, M], U32, name="y_codes", align_bytes=64)
+        y_scales = keep.tile([P, HALVES, M], U8, name="y_scales", align_bytes=64)
+        a_codes = keep.tile([P, GROUPS, M], U32, name="a_codes", align_bytes=64)
+        a_scales = keep.tile([P, GROUPS, M], U8, name="a_scales", align_bytes=64)
+        words_b = keep.tile([P, HALVES, 2 * N], U8, name="words_b", align_bytes=64)
+        scales_b = keep.tile([P, HALVES, N], U8, name="scales_b", align_bytes=64)
+        a_col_scale = keep.tile([P, M], F32, name="a_col_scale", align_bytes=64)
+        code_bytes = [
+            keep.tile([P, 4, M], U8, name="code_bytes%d" % g, align_bytes=64) for g in range(GROUPS)
+        ]
+
+        def bank(i):
+            return psum.tile([P, 512], F32, name="bank%d" % i, tag="bank%d" % i)
+
+        left_rows = {}
+        right_rows = {}
+        d_rows = {}
+        c_rows = {}
+
+        def load_left(g, slots):
+            if slots.start == 0:
+                rows = work.tile([P, 4, K], BF16, name="left_rows", bufs=3, align_bytes=64)
+                left_rows[g] = rows
+            nc.sync.dma_start(
+                out=left_rows[g][:, slots, :],
+                in_=left[512 * g : 512 * g + 512, :].rearrange("(p t) k -> p t k", t=4)[:, slots, :],
+            )
+
+        def load_right(h):
+            rows = work.tile([P, 4, 512], BF16, name="right_rows", bufs=2, align_bytes=64)
+            right_rows[h] = rows
+            nc.sync.dma_start(
+                out=rows[:], in_=right.rearrange("(p t) n -> p t n", t=4)[:, :, 512 * h : 512 * h + 512]
+            )
+
+        def load_field(src, keepers, g):
+            rows = work.tile([P, 4, N], BF16, name="field_rows", bufs=4, align_bytes=64)
+            keepers[g] = rows
+            nc.sync.dma_start(
+                out=rows[:], in_=src[512 * g : 512 * g + 512, :].rearrange("(p t) n -> p t n", t=4)
+            )
+
+        def load_a(pair):
+            g, half = pair // 2, pair % 2
+            nc.sync.dma_start(
+                out=code_bytes[g][:, 2 * half : 2 * half + 2, :],
+                in_=a_bytes[512 * g : 512 * g + 512, :].rearrange("(p t) k -> p t k", t=4)[
+                    :, 2 * half : 2 * half + 2, :
+                ],
+            )
+
+        def load_a_scale():
+            nc.sync.dma_start(
+                out=a_col_scale[:], in_=a_scale.rearrange("o k -> (o k)").partition_broadcast(P)
+            )
+
+        def load_b():
+            nc.sync.dma_start(out=words_b[:], in_=b_words.rearrange("h p n -> p h n"))
+            for q in range(4):
+                nc.sync.dma_start(
+                    out=scales_b[32 * q : 32 * q + 4, :, :].bitcast(I32),
+                    in_=b_scales[:, 4 * q : 4 * q + 4, :].rearrange("h r n -> r h n").bitcast(I32),
+                )
+
+        left_banks = {}
+        left_t = {}
+
+        def left_turn(g, tp):
+            ps = bank(6 + tp)
+            left_banks[g, tp] = ps
+            for tt in range(2):
+                words = left_rows[g][:, 2 * tp + tt, :].bitcast(F32)
+                for u in range(2):
+                    at = (2 * tt + u) * P
+                    nc.tensor.transpose(ps[:, at : at + P], words[:, u : K // 2 : 2], ident[:])
+
+        def left_out(g, tp):
+            lt = work.tile([P, 256, 4], BF16, name="left_t", bufs=2, align_bytes=64)
+            left_t[g, tp] = lt
+            copy_words(lt, left_banks[g, tp])
+
+        def copy_words(dst, ps):
+            nc.scalar.copy(
+                out=dst[:].rearrange("p c t -> p (c t)").bitcast(F32).rearrange("p (w r u) -> p w r u", w=2, u=2),
+                in_=ps[:].rearrange("p (w u r) -> p w r u", w=2, u=2),
+            )
+
+        def quantize(codes, scales, src):
+            nc.vector.quantize_mx(
+                out=codes.bitcast(FP8X4), scales=scales, in_=src[:].rearrange("p c t -> p (c t)")
+            )
+
+        def left_quantize(g, tp):
+            at = 512 * g + 256 * tp
+            quantize(left_codes[:, at : at + 256], left_scales[:, at : at + 256], left_t[g, tp])
+
+        right_t = {}
+
+        def right_interleave(h, u, eng_copy):
+            rt = work.tile([P, 256, 4], BF16, name="right_t", bufs=4, align_bytes=64)
+            right_t[h, u] = rt
+            eng_copy(
+                out=rt[:].rearrange("p (q e) t -> p q e t", e=2),
+                in_=right_rows[h][:].rearrange("p t (q u e) -> p u q e t", u=2, e=2)[:, u],
+            )
+
+        def right_quantize(h, u):
+            cols = slice(512 * h + 256 * u, 512 * h + 256 * u + 256)
+            quantize(right_codes[:, cols], right_scales[:, cols], right_t[h, u])
+
+        x_banks = {}
+        x_t = {}
+        y_rows = {}
+        y_banks = {}
+        y_t = {}
+
+        def x_matmul(j, s):
+            g, h = j // 2, j % 2
+            ps = bank(s)
+            x_banks[j, s] = ps
+            cols = slice(512 * h + 128 * s, 512 * h + 128 * s + 128)
+            for t in range(4):
+                rows = slice(512 * g + 128 * t, 512 * g + 128 * t + 128)
+                nc.tensor.matmul_mx(
+                    out=ps[:, 128 * t : 128 * t + 128],
+                    lhsT=left_codes[:, rows].bitcast(FP8X4),
+                    lhsT_scale=left_scales[:, rows],
+                    rhs=right_codes[:, cols].bitcast(FP8X4),
+                    rhs_scale=right_scales[:, cols],
+                    start=True,
+                    stop=True,
+                )
+
+        def x_out(j, s):
+            if s == 0:
+                xt_new = work.tile([P, 512, 4], BF16, name="x_t", bufs=2, align_bytes=64)
+                x_t[j] = xt_new
+            u, half = s // 2, s % 2
+            nc.scalar.copy(
+                out=x_t[j][:].rearrange("p (q u e) t -> p u q e t", u=2, e=2)[:, u, 64 * half : 64 * half + 64],
+                in_=x_banks[j, s][:].rearrange("p (t q e) -> p q e t", t=4, e=2),
+            )
+
+        def y_multiply(j, s):
+            if s == 0:
+                y_new = work.tile([P, 4, 2, 256], BF16, name="y_rows", bufs=2, align_bytes=64)
+                y_rows[j] = y_new
+            g, h = j // 2, j % 2
+            u, half = s // 2, s % 2
+            nc.vector.tensor_tensor(
+                out=y_rows[j][:, :, u, 128 * half : 128 * half + 128].rearrange("p t (q e) -> p t q e", e=2),
+                in0=x_banks[j, s][:].rearrange("p (t q e) -> p t q e", t=4, e=2),
+                in1=d_rows[g][:, :, 512 * h : 512 * h + 512].rearrange("p t (q u e) -> p u t q e", u=2, e=2)[
+                    :, u, :, 64 * half : 64 * half + 64
+                ],
+                op=MULT,
+            )
+
+        def x_quantize(j):
+            g, h = j // 2, j % 2
+            cols = slice(512 * h, 512 * h + 512)
+            quantize(x_codes[:, g, cols], x_scales[:, g, cols], x_t[j])
+
+        def y_turn(j, tp):
+            ps = bank(6 + tp)
+            y_banks[j, tp] = ps
+            for tt in range(2):
+                for u in range(2):
+                    at = (2 * tt + u) * P
+                    nc.tensor.transpose(
+                        ps[:, at : at + P], y_rows[j][:, 2 * tp + tt, u, :].bitcast(F32), ident[:]
+                    )
+
+        def y_out(j, tp):
+            yt = work.tile([P, 256, 4], BF16, name="y_t", bufs=4, align_bytes=64)
+            y_t[j, tp] = yt
+            copy_words(yt, y_banks[j, tp])
+
+        def y_quantize(j, tp):
+            g, h = j // 2, j % 2
+            at = 512 * g + 256 * tp
+            quantize(y_codes[:, h, at : at + 256], y_scales[:, h, at : at + 256], y_t[j, tp])
+
+        a_values = {}
+        a_words = {}
+        a_banks = {}
+        a_t = {}
+
+        def a_scale_tile(i):
+            vals = work.tile([P, M], BF16, name="a_values", bufs=2, align_bytes=64)
+            a_values[i] = vals
+            nc.vector.tensor_tensor(
+                out=vals[:], in0=code_bytes[i // 4][:, i % 4, :].bitcast(FP8), in1=a_col_scale[:], op=MULT
+            )
+
+        def a_reorder(i):
+            wd = work.tile([P, GROUPS, 2, P], F32, name="a_words", bufs=4, align_bytes=64)
+            a_words[i] = wd
+            nc.scalar.copy(
+                out=wd[:],
+                in_=a_values[i][:].bitcast(F32).rearrange("p (g q u) -> p g u q", g=GROUPS, u=2),
+            )
+
+        def a_turn(k):
+            pair, g = k // 3, k % 3
+            ps = bank(TURN_BANKS[k % 4])
+            a_banks[k] = ps
+            for tt in range(2):
+                for u in range(2):
+                    at = (2 * tt + u) * P
+                    nc.tensor.transpose(ps[:, at : at + P], a_words[2 * pair + tt][:, g, u, :], ident[:])
+
+        def a_out(k):
+            at_new = work.tile([P, 256, 4], BF16, name="a_t", bufs=4, align_bytes=64)
+            a_t[k] = at_new
+            copy_words(at_new, a_banks[k])
+
+        def a_quantize(k):
+            pair, g = k // 3, k % 3
+            cols = slice(256 * pair, 256 * pair + 256)
+            quantize(a_codes[:, g, cols], a_scales[:, g, cols], a_t[k])
+
+        acc = {}
+        results = {}
+
+        def acc_open(i, n):
+            acc[i, n] = bank(ACC_BANKS[(2 * i + n) % 4])
+
+        def pass_yb(i, n, h):
+            rows = slice(P * i, P * i + P)
+            nc.tensor.matmul_mx(
+                out=acc[i, n][:],
+                lhsT=y_codes[:, h, rows].bitcast(FP8X4),
+                lhsT_scale=y_scales[:, h, rows],
+                rhs=words_b[:, h, 1024 * n : 1024 * n + 1024].bitcast(FP4X4),
+                rhs_scale=scales_b[:, h, 512 * n : 512 * n + 512],
+                start=(h == 0),
+                stop=False,
+            )
+
+        def pass_ax(i, n, g):
+            rows = slice(P * i, P * i + P)
+            cols = slice(512 * n, 512 * n + 512)
+            nc.tensor.matmul_mx(
+                out=acc[i, n][:],
+                lhsT=a_codes[:, g, rows].bitcast(FP8X4),
+                lhsT_scale=a_scales[:, g, rows],
+                rhs=x_codes[:, g, cols].bitcast(FP8X4),
+                rhs_scale=x_scales[:, g, cols],
+                start=False,
+                stop=(g == GROUPS - 1),
+            )
+
+        def tile_matmuls(i):
+            acc_open(i, 0)
+            acc_open(i, 1)
+            if i == TILES - 1:
+                for n in range(2):
+                    for h in range(HALVES):
+                        pass_yb(i, n, h)
+                    for g in range(GROUPS):
+                        pass_ax(i, n, g)
+            else:
+                for h in range(HALVES):
+                    for n in range(2):
+                        pass_yb(i, n, h)
+                for g in range(GROUPS):
+                    for n in range(2):
+                        pass_ax(i, n, g)
+
+        def subtract_c(i, n):
+            if n == 0:
+                res = work.tile([P, N], F32, name="result", bufs=4, align_bytes=64)
+                results[i] = res
+            g, t = i // 4, i % 4
+            cols = slice(512 * n, 512 * n + 512)
+            nc.vector.tensor_tensor(
+                out=results[i][:, cols], in0=acc[i, n][:], in1=c_rows[g][:, t, cols], op=SUB
+            )
+
+        def store(i, n):
+            g, t = i // 4, i % 4
+            rows = out[512 * g : 512 * g + 512, :].rearrange("(p t) n -> p t n", t=4)[:, t, :]
+            if n is None:
+                nc.sync.dma_start(out=rows, in_=results[i][:])
+            else:
+                cols = slice(512 * n, 512 * n + 512)
+                nc.sync.dma_start(out=rows[:, cols], in_=results[i][:, cols])
+
+        def finish(i):
+            subtract_c(i, 0)
+            if i == TILES - 1:
+                store(i, 0)
+            subtract_c(i, 1)
+            store(i, 1 if i == TILES - 1 else None)
+
+        make_identity(nc, ident[:])
+        with tc.manual_schedule():
+            load_left(0, slice(0, 2))
+            load_left(0, slice(2, 4))
+            load_right(0)
+            load_right(1)
+            load_field(d, d_rows, 0)
+            load_left(1, slice(0, 4))
+            load_a_scale()
+            load_a(0)
+            load_left(2, slice(0, 4))
+            load_field(d, d_rows, 1)
+            nc.vector.memset(scales_b[:].rearrange("p h n -> p (h n)").bitcast(I32), 0)
+            load_a(1)
+            load_b()
+            load_field(d, d_rows, 2)
+            load_a(2)
+            load_field(c, c_rows, 0)
+            load_a(3)
+            load_a(4)
+            load_a(5)
+
+            for tp in range(2):
+                left_turn(0, tp)
+            for tp in range(2):
+                left_out(0, tp)
+            right_interleave(0, 0, nc.vector.tensor_copy)
+            left_quantize(0, 0)
+            right_quantize(0, 0)
+            left_quantize(0, 1)
+            right_interleave(0, 1, nc.vector.tensor_copy)
+            right_interleave(1, 0, nc.scalar.copy)
+            right_quantize(0, 1)
+
+            for j in range(7):
+                g, h = j // 2, j % 2
+                live = j < 6
+                turn_left = live and h == 0 and g + 1 < GROUPS
+                if live:
+                    x_matmul(j, 0)
+                    x_matmul(j, 1)
+                    x_out(j, 0)
+                    y_multiply(j, 0)
+                if j > 0:
+                    y_turn(j - 1, 0)
+                    y_turn(j - 1, 1)
+                    y_out(j - 1, 0)
+                    x_quantize(j - 1)
+                if live:
+                    x_matmul(j, 2)
+                    x_matmul(j, 3)
+                    x_out(j, 1)
+                    y_multiply(j, 1)
+                if j == 0:
+                    right_interleave(1, 1, nc.vector.tensor_copy)
+                    right_quantize(1, 0)
+                    right_quantize(1, 1)
+                if j > 0:
+                    y_out(j - 1, 1)
+                    y_quantize(j - 1, 0)
+                if live:
+                    x_out(j, 2)
+                    y_multiply(j, 2)
+                if j > 0:
+                    y_quantize(j - 1, 1)
+                if turn_left:
+                    left_turn(g + 1, 0)
+                    left_turn(g + 1, 1)
+                    left_out(g + 1, 0)
+                if live:
+                    x_out(j, 3)
+                    y_multiply(j, 3)
+                if turn_left:
+                    left_out(g + 1, 1)
+                    left_quantize(g + 1, 0)
+                    left_quantize(g + 1, 1)
+                if j in (1, 3):
+                    load_field(c, c_rows, (j + 1) // 2)
+                if 2 <= j <= 5:
+                    a_reorder(j - 2)
+                if 1 <= j <= 4:
+                    a_scale_tile(j - 1)
+                if j == 5:
+                    for k in range(3):
+                        a_turn(k)
+                        a_out(k)
+                    for k in range(3):
+                        a_quantize(k)
+
+            pairs = TILES // 2
+            for p in range(pairs):
+                if p + 1 < pairs:
+                    for k in range(3 * p + 3, 3 * p + 6):
+                        a_turn(k)
+                        a_out(k)
+                tile_matmuls(2 * p)
+                if p + 2 < pairs:
+                    a_scale_tile(2 * p + 4)
+                    a_reorder(2 * p + 4)
+                if p > 0:
+                    finish(2 * p - 1)
+                if p + 1 < pairs:
+                    for k in range(3 * p + 3, 3 * p + 6):
+                        a_quantize(k)
+                tile_matmuls(2 * p + 1)
+                if p + 2 < pairs:
+                    a_scale_tile(2 * p + 5)
+                    a_reorder(2 * p + 5)
+                finish(2 * p)
+            finish(TILES - 1)

@@ -20,8 +20,6 @@ SUB = mybir.AluOpType.subtract
 P = 128
 GROUPS = M // 512
 HALVES = N // 512
-TURN_BANKS = (6, 7, 0, 1)
-ACC_BANKS = (4, 5, 2, 3)
 TILES = M // P
 
 
@@ -52,45 +50,65 @@ def tile_sylvester_scaled_residual_s8_kernel(
             keep.tile([P, 4, M], U8, name="code_bytes%d" % g, align_bytes=64) for g in range(GROUPS)
         ]
 
-        def bank(i):
-            return psum.tile([P, 512], F32, name="bank%d" % i, tag="bank%d" % i)
+        free_banks = list(range(8))
+        banks = {}
+        bank_of = {}
+        tiles = {}
 
-        left_rows = {}
-        right_rows = {}
-        d_rows = {}
-        c_rows = {}
+        def take_bank(key):
+            b = free_banks.pop(0)
+            bank_of[key] = b
+            ps = psum.tile([P, 512], F32, name="bank%d" % b, tag="bank%d" % b)
+            banks[key] = ps
+            return ps
 
-        def load_left(g, slots):
-            if slots.start == 0:
-                rows = work.tile([P, 4, K], BF16, name="left_rows", bufs=3, align_bytes=64)
-                left_rows[g] = rows
-            nc.sync.dma_start(
-                out=left_rows[g][:, slots, :],
-                in_=left[512 * g : 512 * g + 512, :].rearrange("(p t) k -> p t k", t=4)[:, slots, :],
+        def drop_bank(key):
+            free_banks.append(bank_of[key])
+
+        def work_tile(key, shape, dtype, name, bufs):
+            new = work.tile(shape, dtype, name=name, bufs=bufs, align_bytes=64)
+            tiles[key] = new
+            return new
+
+        def quantize(codes, scales, src):
+            nc.vector.quantize_mx(
+                out=codes.bitcast(FP8X4), scales=scales, in_=src[:].rearrange("p c t -> p (c t)")
             )
 
+        def turn(ps, at, words):
+            nc.tensor.transpose(ps[:, at : at + P], words, ident[:])
+
+        def copy_words(dst, ps):
+            nc.scalar.copy(
+                out=dst[:].rearrange("p c t -> p (c t)").bitcast(F32).rearrange("p (w r u) -> p w r u", w=2, u=2),
+                in_=ps[:].rearrange("p (w u r) -> p w r u", w=2, u=2),
+            )
+
+        def rows_view(src, g):
+            return src[512 * g : 512 * g + 512, :].rearrange("(p t) n -> p t n", t=4)
+
+        def load_left(g, lo, hi):
+            if lo == 0:
+                work_tile(("left", g), [P, 4, K], BF16, "left_rows", 3)
+            nc.sync.dma_start(out=tiles["left", g][:, lo:hi, :], in_=rows_view(left, g)[:, lo:hi, :])
+
         def load_right(h):
-            rows = work.tile([P, 4, 512], BF16, name="right_rows", bufs=2, align_bytes=64)
-            right_rows[h] = rows
+            rows = work_tile(("right", h), [P, 4, 512], BF16, "right_rows", 2)
             nc.sync.dma_start(
                 out=rows[:], in_=right.rearrange("(p t) n -> p t n", t=4)[:, :, 512 * h : 512 * h + 512]
             )
 
-        def load_field(src, keepers, g):
-            rows = work.tile([P, 4, N], BF16, name="field_rows", bufs=4, align_bytes=64)
-            keepers[g] = rows
-            nc.sync.dma_start(
-                out=rows[:], in_=src[512 * g : 512 * g + 512, :].rearrange("(p t) n -> p t n", t=4)
-            )
+        def load_d(g):
+            rows = work_tile(("d", g), [P, 4, N], BF16, "field_rows", 4)
+            nc.sync.dma_start(out=rows[:], in_=rows_view(d, g))
+
+        def load_c(g):
+            rows = work_tile(("c", g), [P, 4, N], BF16, "field_rows", 4)
+            nc.sync.dma_start(out=rows[:], in_=rows_view(c, g))
 
         def load_a(pair):
-            g, half = pair // 2, pair % 2
-            nc.sync.dma_start(
-                out=code_bytes[g][:, 2 * half : 2 * half + 2, :],
-                in_=a_bytes[512 * g : 512 * g + 512, :].rearrange("(p t) k -> p t k", t=4)[
-                    :, 2 * half : 2 * half + 2, :
-                ],
-            )
+            g, t = pair // 2, 2 * (pair % 2)
+            nc.sync.dma_start(out=code_bytes[g][:, t : t + 2, :], in_=rows_view(a_bytes, g)[:, t : t + 2, :])
 
         def load_a_scale():
             nc.sync.dma_start(
@@ -105,67 +123,54 @@ def tile_sylvester_scaled_residual_s8_kernel(
                     in_=b_scales[:, 4 * q : 4 * q + 4, :].rearrange("h r n -> r h n").bitcast(I32),
                 )
 
-        left_banks = {}
-        left_t = {}
+        def clear_b_scales():
+            nc.vector.memset(scales_b[:].rearrange("p h n -> p (h n)").bitcast(I32), 0)
+
+        def store(i, n0, n1):
+            nc.sync.dma_start(out=rows_view(out, i // 4)[:, i % 4, n0:n1], in_=tiles["result", i][:, n0:n1])
 
         def left_turn(g, tp):
-            ps = bank(6 + tp)
-            left_banks[g, tp] = ps
+            ps = take_bank(("left", g, tp))
             for tt in range(2):
-                words = left_rows[g][:, 2 * tp + tt, :].bitcast(F32)
+                words = tiles["left", g][:, 2 * tp + tt, :].bitcast(F32)
                 for u in range(2):
-                    at = (2 * tt + u) * P
-                    nc.tensor.transpose(ps[:, at : at + P], words[:, u : K // 2 : 2], ident[:])
+                    turn(ps, (2 * tt + u) * P, words[:, u : K // 2 : 2])
 
         def left_out(g, tp):
-            lt = work.tile([P, 256, 4], BF16, name="left_t", bufs=2, align_bytes=64)
-            left_t[g, tp] = lt
-            copy_words(lt, left_banks[g, tp])
-
-        def copy_words(dst, ps):
-            nc.scalar.copy(
-                out=dst[:].rearrange("p c t -> p (c t)").bitcast(F32).rearrange("p (w r u) -> p w r u", w=2, u=2),
-                in_=ps[:].rearrange("p (w u r) -> p w r u", w=2, u=2),
-            )
-
-        def quantize(codes, scales, src):
-            nc.vector.quantize_mx(
-                out=codes.bitcast(FP8X4), scales=scales, in_=src[:].rearrange("p c t -> p (c t)")
-            )
+            copy_words(work_tile(("left_t", g, tp), [P, 256, 4], BF16, "left_t", 2), banks["left", g, tp])
+            drop_bank(("left", g, tp))
 
         def left_quantize(g, tp):
             at = 512 * g + 256 * tp
-            quantize(left_codes[:, at : at + 256], left_scales[:, at : at + 256], left_t[g, tp])
+            quantize(left_codes[:, at : at + 256], left_scales[:, at : at + 256], tiles["left_t", g, tp])
 
-        right_t = {}
-
-        def right_interleave(h, u, eng_copy):
-            rt = work.tile([P, 256, 4], BF16, name="right_t", bufs=4, align_bytes=64)
-            right_t[h, u] = rt
-            eng_copy(
+        def right_interleave(h, u):
+            rt = work_tile(("right_t", h, u), [P, 256, 4], BF16, "right_t", 4)
+            copy = nc.scalar.copy if (h, u) == (1, 0) else nc.vector.tensor_copy
+            copy(
                 out=rt[:].rearrange("p (q e) t -> p q e t", e=2),
-                in_=right_rows[h][:].rearrange("p t (q u e) -> p u q e t", u=2, e=2)[:, u],
+                in_=tiles["right", h][:].rearrange("p t (q u e) -> p u q e t", u=2, e=2)[:, u],
             )
 
         def right_quantize(h, u):
             cols = slice(512 * h + 256 * u, 512 * h + 256 * u + 256)
-            quantize(right_codes[:, cols], right_scales[:, cols], right_t[h, u])
+            quantize(right_codes[:, cols], right_scales[:, cols], tiles["right_t", h, u])
 
-        x_banks = {}
-        x_t = {}
-        y_rows = {}
-        y_banks = {}
-        y_t = {}
+        x_reads = {}
+
+        def x_read(j, s):
+            x_reads[j, s] = x_reads.get((j, s), 0) + 1
+            if x_reads[j, s] == 2:
+                drop_bank(("x", j, s))
 
         def x_matmul(j, s):
             g, h = j // 2, j % 2
-            ps = bank(s)
-            x_banks[j, s] = ps
-            cols = slice(512 * h + 128 * s, 512 * h + 128 * s + 128)
+            ps = take_bank(("x", j, s))
+            cols = slice(512 * h + P * s, 512 * h + P * s + P)
             for t in range(4):
-                rows = slice(512 * g + 128 * t, 512 * g + 128 * t + 128)
+                rows = slice(512 * g + P * t, 512 * g + P * t + P)
                 nc.tensor.matmul_mx(
-                    out=ps[:, 128 * t : 128 * t + 128],
+                    out=ps[:, P * t : P * t + P],
                     lhsT=left_codes[:, rows].bitcast(FP8X4),
                     lhsT_scale=left_scales[:, rows],
                     rhs=right_codes[:, cols].bitcast(FP8X4),
@@ -176,274 +181,200 @@ def tile_sylvester_scaled_residual_s8_kernel(
 
         def x_out(j, s):
             if s == 0:
-                xt_new = work.tile([P, 512, 4], BF16, name="x_t", bufs=2, align_bytes=64)
-                x_t[j] = xt_new
+                work_tile(("x_t", j), [P, 512, 4], BF16, "x_t", 2)
             u, half = s // 2, s % 2
             nc.scalar.copy(
-                out=x_t[j][:].rearrange("p (q u e) t -> p u q e t", u=2, e=2)[:, u, 64 * half : 64 * half + 64],
-                in_=x_banks[j, s][:].rearrange("p (t q e) -> p q e t", t=4, e=2),
+                out=tiles["x_t", j][:].rearrange("p (q u e) t -> p u q e t", u=2, e=2)[:, u, 64 * half : 64 * half + 64],
+                in_=banks["x", j, s][:].rearrange("p (t q e) -> p q e t", t=4, e=2),
             )
+            x_read(j, s)
+
+        def x_quantize(j):
+            g, cols = j // 2, slice(512 * (j % 2), 512 * (j % 2) + 512)
+            quantize(x_codes[:, g, cols], x_scales[:, g, cols], tiles["x_t", j])
 
         def y_multiply(j, s):
             if s == 0:
-                y_new = work.tile([P, 4, 2, 256], BF16, name="y_rows", bufs=2, align_bytes=64)
-                y_rows[j] = y_new
+                work_tile(("y_rows", j), [P, 4, 2, 256], BF16, "y_rows", 3)
             g, h = j // 2, j % 2
             u, half = s // 2, s % 2
             nc.vector.tensor_tensor(
-                out=y_rows[j][:, :, u, 128 * half : 128 * half + 128].rearrange("p t (q e) -> p t q e", e=2),
-                in0=x_banks[j, s][:].rearrange("p (t q e) -> p t q e", t=4, e=2),
-                in1=d_rows[g][:, :, 512 * h : 512 * h + 512].rearrange("p t (q u e) -> p u t q e", u=2, e=2)[
+                out=tiles["y_rows", j][:, :, u, P * half : P * half + P].rearrange("p t (q e) -> p t q e", e=2),
+                in0=banks["x", j, s][:].rearrange("p (t q e) -> p t q e", t=4, e=2),
+                in1=tiles["d", g][:, :, 512 * h : 512 * h + 512].rearrange("p t (q u e) -> p u t q e", u=2, e=2)[
                     :, u, :, 64 * half : 64 * half + 64
                 ],
                 op=MULT,
             )
-
-        def x_quantize(j):
-            g, h = j // 2, j % 2
-            cols = slice(512 * h, 512 * h + 512)
-            quantize(x_codes[:, g, cols], x_scales[:, g, cols], x_t[j])
+            x_read(j, s)
 
         def y_turn(j, tp):
-            ps = bank(6 + tp)
-            y_banks[j, tp] = ps
+            ps = take_bank(("y", j, tp))
             for tt in range(2):
                 for u in range(2):
-                    at = (2 * tt + u) * P
-                    nc.tensor.transpose(
-                        ps[:, at : at + P], y_rows[j][:, 2 * tp + tt, u, :].bitcast(F32), ident[:]
-                    )
+                    turn(ps, (2 * tt + u) * P, tiles["y_rows", j][:, 2 * tp + tt, u, :].bitcast(F32))
 
         def y_out(j, tp):
-            yt = work.tile([P, 256, 4], BF16, name="y_t", bufs=4, align_bytes=64)
-            y_t[j, tp] = yt
-            copy_words(yt, y_banks[j, tp])
+            copy_words(work_tile(("y_t", j, tp), [P, 256, 4], BF16, "y_t", 4), banks["y", j, tp])
+            drop_bank(("y", j, tp))
 
         def y_quantize(j, tp):
             g, h = j // 2, j % 2
             at = 512 * g + 256 * tp
-            quantize(y_codes[:, h, at : at + 256], y_scales[:, h, at : at + 256], y_t[j, tp])
+            quantize(y_codes[:, h, at : at + 256], y_scales[:, h, at : at + 256], tiles["y_t", j, tp])
 
-        a_values = {}
-        a_words = {}
-        a_banks = {}
-        a_t = {}
-
-        def a_scale_tile(i):
-            vals = work.tile([P, M], BF16, name="a_values", bufs=2, align_bytes=64)
-            a_values[i] = vals
+        def a_multiply(i):
+            vals = work_tile(("a_values", i), [P, M], BF16, "a_values", 2)
             nc.vector.tensor_tensor(
                 out=vals[:], in0=code_bytes[i // 4][:, i % 4, :].bitcast(FP8), in1=a_col_scale[:], op=MULT
             )
 
         def a_reorder(i):
-            wd = work.tile([P, GROUPS, 2, P], F32, name="a_words", bufs=4, align_bytes=64)
-            a_words[i] = wd
             nc.scalar.copy(
-                out=wd[:],
-                in_=a_values[i][:].bitcast(F32).rearrange("p (g q u) -> p g u q", g=GROUPS, u=2),
+                out=work_tile(("a_words", i), [P, GROUPS, 2, P], F32, "a_words", 4)[:],
+                in_=tiles["a_values", i][:].bitcast(F32).rearrange("p (g q u) -> p g u q", g=GROUPS, u=2),
             )
 
-        def a_turn(k):
-            pair, g = k // 3, k % 3
-            ps = bank(TURN_BANKS[k % 4])
-            a_banks[k] = ps
+        def a_turn(pair, g):
+            ps = take_bank(("a", pair, g))
             for tt in range(2):
                 for u in range(2):
-                    at = (2 * tt + u) * P
-                    nc.tensor.transpose(ps[:, at : at + P], a_words[2 * pair + tt][:, g, u, :], ident[:])
+                    turn(ps, (2 * tt + u) * P, tiles["a_words", 2 * pair + tt][:, g, u, :])
 
-        def a_out(k):
-            at_new = work.tile([P, 256, 4], BF16, name="a_t", bufs=4, align_bytes=64)
-            a_t[k] = at_new
-            copy_words(at_new, a_banks[k])
+        def a_out(pair, g):
+            copy_words(work_tile(("a_t", pair, g), [P, 256, 4], BF16, "a_t", 4), banks["a", pair, g])
+            drop_bank(("a", pair, g))
 
-        def a_quantize(k):
-            pair, g = k // 3, k % 3
+        def a_quantize(pair, g):
             cols = slice(256 * pair, 256 * pair + 256)
-            quantize(a_codes[:, g, cols], a_scales[:, g, cols], a_t[k])
+            quantize(a_codes[:, g, cols], a_scales[:, g, cols], tiles["a_t", pair, g])
 
-        acc = {}
-        results = {}
+        passes = {}
 
-        def acc_open(i, n):
-            acc[i, n] = bank(ACC_BANKS[(2 * i + n) % 4])
+        def open_pass(i, n):
+            passes[i, n] = passes.get((i, n), 0) + 1
+            if passes[i, n] == 1:
+                take_bank(("out", i, n))
+            return dict(
+                out=banks["out", i, n][:], start=(passes[i, n] == 1), stop=(passes[i, n] == HALVES + GROUPS)
+            )
 
-        def pass_yb(i, n, h):
+        def y_pass(i, n, h):
             rows = slice(P * i, P * i + P)
             nc.tensor.matmul_mx(
-                out=acc[i, n][:],
                 lhsT=y_codes[:, h, rows].bitcast(FP8X4),
                 lhsT_scale=y_scales[:, h, rows],
                 rhs=words_b[:, h, 1024 * n : 1024 * n + 1024].bitcast(FP4X4),
                 rhs_scale=scales_b[:, h, 512 * n : 512 * n + 512],
-                start=(h == 0),
-                stop=False,
+                **open_pass(i, n),
             )
 
-        def pass_ax(i, n, g):
+        def a_pass(i, n, g):
             rows = slice(P * i, P * i + P)
             cols = slice(512 * n, 512 * n + 512)
             nc.tensor.matmul_mx(
-                out=acc[i, n][:],
                 lhsT=a_codes[:, g, rows].bitcast(FP8X4),
                 lhsT_scale=a_scales[:, g, rows],
                 rhs=x_codes[:, g, cols].bitcast(FP8X4),
                 rhs_scale=x_scales[:, g, cols],
-                start=False,
-                stop=(g == GROUPS - 1),
+                **open_pass(i, n),
             )
-
-        def tile_matmuls(i):
-            acc_open(i, 0)
-            acc_open(i, 1)
-            if i == TILES - 1:
-                for n in range(2):
-                    for h in range(HALVES):
-                        pass_yb(i, n, h)
-                    for g in range(GROUPS):
-                        pass_ax(i, n, g)
-            else:
-                for h in range(HALVES):
-                    for n in range(2):
-                        pass_yb(i, n, h)
-                for g in range(GROUPS):
-                    for n in range(2):
-                        pass_ax(i, n, g)
 
         def subtract_c(i, n):
             if n == 0:
-                res = work.tile([P, N], F32, name="result", bufs=4, align_bytes=64)
-                results[i] = res
-            g, t = i // 4, i % 4
+                work_tile(("result", i), [P, N], F32, "result", 4)
             cols = slice(512 * n, 512 * n + 512)
             nc.vector.tensor_tensor(
-                out=results[i][:, cols], in0=acc[i, n][:], in1=c_rows[g][:, t, cols], op=SUB
+                out=tiles["result", i][:, cols],
+                in0=banks["out", i, n][:],
+                in1=tiles["c", i // 4][:, i % 4, cols],
+                op=SUB,
             )
+            drop_bank(("out", i, n))
 
-        def store(i, n):
-            g, t = i // 4, i % 4
-            rows = out[512 * g : 512 * g + 512, :].rearrange("(p t) n -> p t n", t=4)[:, t, :]
-            if n is None:
-                nc.sync.dma_start(out=rows, in_=results[i][:])
-            else:
-                cols = slice(512 * n, 512 * n + 512)
-                nc.sync.dma_start(out=rows[:, cols], in_=results[i][:, cols])
+        def needs(step):
+            f, x = step[0], step[1:]
+            if f == left_turn:
+                return [(load_left, 0, 2 * x[1], 2 * x[1] + 2)] if x[0] == 0 else [(load_left, x[0], 0, 4)]
+            if f == left_out:
+                n = 2 * x[0] + x[1] - 2
+                return [(left_turn,) + x] + ([(left_quantize, n // 2, n % 2)] if n >= 0 else [])
+            if f == left_quantize:
+                return [(left_out,) + x]
+            if f == right_interleave:
+                return [(load_right, x[0])]
+            if f == right_quantize:
+                return [(right_interleave,) + x]
+            if f == x_matmul:
+                return [(left_quantize, x[0] // 2, tp) for tp in range(2)] + [(right_quantize, x[0] % 2, x[1] // 2)]
+            if f == x_out:
+                return [(x_matmul,) + x] + ([(x_quantize, x[0] - 2)] if x[0] > 1 else [])
+            if f == y_multiply:
+                return [(x_matmul,) + x, (load_d, x[0] // 2)] + ([(y_turn, x[0] - 3, 1)] if x[0] > 2 else [])
+            if f == x_quantize:
+                return [(x_out, x[0], s) for s in range(4)]
+            if f == y_turn:
+                return [(y_multiply, x[0], s) for s in range(4)]
+            if f == y_out:
+                return [(y_turn,) + x] + ([(y_quantize, x[0] - 2, x[1])] if x[0] > 1 else [])
+            if f == y_quantize:
+                return [(y_out,) + x]
+            if f == a_multiply:
+                return [(load_a_scale,), (load_a, x[0] // 2)] + ([(a_reorder, x[0] - 2)] if x[0] > 1 else [])
+            if f == a_reorder:
+                return [(a_multiply,) + x] + ([(a_turn, x[0] // 2 - 2, GROUPS - 1)] if x[0] > 3 else [])
+            if f == a_turn:
+                return [(a_reorder, 2 * x[0] + tt) for tt in range(2)]
+            if f == a_out:
+                n = 3 * x[0] + x[1] - 4
+                return [(a_turn,) + x] + ([(a_quantize, n // 3, n % 3)] if n >= 0 else [])
+            if f == a_quantize:
+                return [(a_out,) + x]
+            if f == y_pass:
+                return [(y_quantize, 2 * (x[0] // 4) + x[2], x[0] % 4 // 2), (load_b,)]
+            if f == a_pass:
+                return [(a_quantize, x[0] // 2, x[2]), (x_quantize, 2 * x[2] + x[1])]
+            if f == subtract_c:
+                return (
+                    [(y_pass,) + x + (h,) for h in range(HALVES)]
+                    + [(a_pass,) + x + (g,) for g in range(GROUPS)]
+                    + [(load_c, x[0] // 4)]
+                    + ([(store, x[0] - 4, 0, N)] if x[0] > 3 else [])
+                )
+            if f == store:
+                return [(subtract_c, x[0], n) for n in range(x[1] // 512, x[2] // 512)]
+            if f == load_b:
+                return [(clear_b_scales,)]
+            if f == load_c and x[0] > 0:
+                return [(y_multiply, 2 * x[0] - 1, 3)]
+            return []
 
-        def finish(i):
-            subtract_c(i, 0)
-            if i == TILES - 1:
-                store(i, 0)
-            subtract_c(i, 1)
-            store(i, 1 if i == TILES - 1 else None)
+        TAKES_BANK = (left_turn, x_matmul, y_turn, a_turn)
+
+        def issue(queues):
+            left_over = [list(q) for q in queues]
+            issued = set()
+            while any(left_over):
+                stuck = True
+                for q in left_over:
+                    if not q:
+                        continue
+                    step = q[0]
+                    f, x = step[0], step[1:]
+                    opens = f in TAKES_BANK or (f in (y_pass, a_pass) and x[:2] not in passes)
+                    if (opens and not free_banks) or any(s not in issued for s in needs(step)):
+                        continue
+                    f(*x)
+                    issued.add(step)
+                    q.pop(0)
+                    stuck = False
+                assert not stuck
 
         make_identity(nc, ident[:])
         with tc.manual_schedule():
-            load_left(0, slice(0, 2))
-            load_left(0, slice(2, 4))
-            load_right(0)
-            load_right(1)
-            load_field(d, d_rows, 0)
-            load_left(1, slice(0, 4))
-            load_a_scale()
-            load_a(0)
-            load_left(2, slice(0, 4))
-            load_field(d, d_rows, 1)
-            nc.vector.memset(scales_b[:].rearrange("p h n -> p (h n)").bitcast(I32), 0)
-            load_a(1)
-            load_b()
-            load_field(d, d_rows, 2)
-            load_a(2)
-            load_field(c, c_rows, 0)
-            load_a(3)
-            load_a(4)
-            load_a(5)
-
-            for tp in range(2):
-                left_turn(0, tp)
-            for tp in range(2):
-                left_out(0, tp)
-            right_interleave(0, 0, nc.vector.tensor_copy)
-            left_quantize(0, 0)
-            right_quantize(0, 0)
-            left_quantize(0, 1)
-            right_interleave(0, 1, nc.vector.tensor_copy)
-            right_interleave(1, 0, nc.scalar.copy)
-            right_quantize(0, 1)
-
-            for j in range(7):
-                g, h = j // 2, j % 2
-                live = j < 6
-                turn_left = live and h == 0 and g + 1 < GROUPS
-                if live:
-                    x_matmul(j, 0)
-                    x_matmul(j, 1)
-                    x_out(j, 0)
-                    y_multiply(j, 0)
-                if j > 0:
-                    y_turn(j - 1, 0)
-                    y_turn(j - 1, 1)
-                    y_out(j - 1, 0)
-                    x_quantize(j - 1)
-                if live:
-                    x_matmul(j, 2)
-                    x_matmul(j, 3)
-                    x_out(j, 1)
-                    y_multiply(j, 1)
-                if j == 0:
-                    right_interleave(1, 1, nc.vector.tensor_copy)
-                    right_quantize(1, 0)
-                    right_quantize(1, 1)
-                if j > 0:
-                    y_out(j - 1, 1)
-                    y_quantize(j - 1, 0)
-                if live:
-                    x_out(j, 2)
-                    y_multiply(j, 2)
-                if j > 0:
-                    y_quantize(j - 1, 1)
-                if turn_left:
-                    left_turn(g + 1, 0)
-                    left_turn(g + 1, 1)
-                    left_out(g + 1, 0)
-                if live:
-                    x_out(j, 3)
-                    y_multiply(j, 3)
-                if turn_left:
-                    left_out(g + 1, 1)
-                    left_quantize(g + 1, 0)
-                    left_quantize(g + 1, 1)
-                if j in (1, 3):
-                    load_field(c, c_rows, (j + 1) // 2)
-                if 2 <= j <= 5:
-                    a_reorder(j - 2)
-                if 1 <= j <= 4:
-                    a_scale_tile(j - 1)
-                if j == 5:
-                    for k in range(3):
-                        a_turn(k)
-                        a_out(k)
-                    for k in range(3):
-                        a_quantize(k)
-
-            pairs = TILES // 2
-            for p in range(pairs):
-                if p + 1 < pairs:
-                    for k in range(3 * p + 3, 3 * p + 6):
-                        a_turn(k)
-                        a_out(k)
-                tile_matmuls(2 * p)
-                if p + 2 < pairs:
-                    a_scale_tile(2 * p + 4)
-                    a_reorder(2 * p + 4)
-                if p > 0:
-                    finish(2 * p - 1)
-                if p + 1 < pairs:
-                    for k in range(3 * p + 3, 3 * p + 6):
-                        a_quantize(k)
-                tile_matmuls(2 * p + 1)
-                if p + 2 < pairs:
-                    a_scale_tile(2 * p + 5)
-                    a_reorder(2 * p + 5)
-                finish(2 * p)
-            finish(TILES - 1)
+            issue((
+                [(load_left, 0, 0, 2), (load_left, 0, 2, 4), (load_right, 0), (load_right, 1), (load_left, 1, 0, 4), (load_d, 0), (load_left, 2, 0, 4), (load_a_scale,), (load_a, 0), (load_d, 1), (load_a, 1), (load_d, 2), (load_b,), (load_a, 2), (load_c, 0), (load_c, 1), (load_a, 3), (load_a, 4), (load_a, 5), (load_c, 2), (store, 0, 0, N), (store, 1, 0, N), (store, 2, 0, N), (store, 3, 0, N), (store, 4, 0, N), (store, 5, 0, N), (store, 6, 0, N), (store, 7, 0, N), (store, 8, 0, N), (store, 9, 0, N), (store, 10, 0, N), (store, 11, 0, 512), (store, 11, 512, 1024)],
+                [(left_turn, 0, 0,), (left_turn, 0, 1,), (x_matmul, 0, 0,), (x_matmul, 0, 1,), (left_turn, 1, 0,), (left_turn, 1, 1,), (x_matmul, 0, 2,), (x_matmul, 0, 3,), (x_matmul, 1, 0,), (x_matmul, 1, 1,), (x_matmul, 1, 2,), (x_matmul, 1, 3,), (left_turn, 2, 0,), (left_turn, 2, 1,), (y_turn, 0, 0,), (y_turn, 0, 1,), (x_matmul, 2, 0,), (x_matmul, 2, 1,), (x_matmul, 2, 2,), (x_matmul, 2, 3,), (y_turn, 1, 0,), (y_turn, 1, 1,), (x_matmul, 3, 0,), (x_matmul, 3, 1,), (x_matmul, 3, 2,), (x_matmul, 3, 3,), (x_matmul, 4, 0,), (x_matmul, 4, 1,), (x_matmul, 4, 2,), (x_matmul, 4, 3,), (a_turn, 0, 0,), (a_turn, 0, 1,), (a_turn, 0, 2,), (y_turn, 2, 0,), (y_turn, 2, 1,), (y_pass, 0, 0, 0,), (y_pass, 0, 1, 0,), (y_pass, 0, 0, 1,), (y_pass, 0, 1, 1,), (x_matmul, 5, 0,), (x_matmul, 5, 1,), (x_matmul, 5, 2,), (x_matmul, 5, 3,), (y_pass, 1, 0, 0,), (y_pass, 1, 1, 0,), (y_pass, 1, 0, 1,), (y_pass, 1, 1, 1,), (a_pass, 0, 0, 0,), (a_pass, 0, 1, 0,), (a_pass, 0, 0, 1,), (a_pass, 0, 1, 1,), (a_pass, 1, 0, 0,), (a_pass, 1, 1, 0,), (a_turn, 1, 0,), (a_turn, 1, 1,), (a_turn, 1, 2,), (y_turn, 3, 0,), (y_turn, 3, 1,), (y_turn, 4, 0,), (y_turn, 4, 1,), (a_pass, 0, 0, 2,), (a_pass, 0, 1, 2,), (a_pass, 1, 0, 1,), (a_pass, 1, 1, 1,), (a_pass, 1, 0, 2,), (a_pass, 1, 1, 2,), (y_pass, 2, 0, 0,), (y_pass, 2, 1, 0,), (y_pass, 2, 0, 1,), (y_pass, 2, 1, 1,), (a_pass, 2, 0, 0,), (a_pass, 2, 1, 0,), (a_pass, 2, 0, 1,), (a_pass, 2, 1, 1,), (a_pass, 2, 0, 2,), (a_pass, 2, 1, 2,), (y_pass, 3, 0, 0,), (y_pass, 3, 1, 0,), (y_pass, 3, 0, 1,), (y_pass, 3, 1, 1,), (a_turn, 2, 0,), (a_turn, 2, 1,), (a_turn, 2, 2,), (y_turn, 5, 0,), (y_turn, 5, 1,), (a_pass, 3, 0, 0,), (a_pass, 3, 1, 0,), (a_pass, 3, 0, 1,), (a_pass, 3, 1, 1,), (a_pass, 3, 0, 2,), (a_pass, 3, 1, 2,), (y_pass, 4, 0, 0,), (y_pass, 4, 1, 0,), (y_pass, 4, 0, 1,), (y_pass, 4, 1, 1,), (a_pass, 4, 0, 0,), (a_pass, 4, 1, 0,), (a_pass, 4, 0, 1,), (a_pass, 4, 1, 1,), (a_pass, 4, 0, 2,), (a_pass, 4, 1, 2,), (y_pass, 5, 0, 0,), (y_pass, 5, 1, 0,), (y_pass, 5, 0, 1,), (y_pass, 5, 1, 1,), (a_turn, 3, 0,), (a_turn, 3, 1,), (a_turn, 3, 2,), (a_pass, 5, 0, 0,), (a_pass, 5, 1, 0,), (a_pass, 5, 0, 1,), (a_pass, 5, 1, 1,), (a_pass, 5, 0, 2,), (a_pass, 5, 1, 2,), (y_pass, 6, 0, 0,), (y_pass, 6, 1, 0,), (y_pass, 6, 0, 1,), (y_pass, 6, 1, 1,), (a_pass, 6, 0, 0,), (a_pass, 6, 1, 0,), (a_pass, 6, 0, 1,), (a_pass, 6, 1, 1,), (a_pass, 6, 0, 2,), (a_pass, 6, 1, 2,), (y_pass, 7, 0, 0,), (y_pass, 7, 1, 0,), (y_pass, 7, 0, 1,), (y_pass, 7, 1, 1,), (a_turn, 4, 0,), (a_turn, 4, 1,), (a_turn, 4, 2,), (a_pass, 7, 0, 0,), (a_pass, 7, 1, 0,), (a_pass, 7, 0, 1,), (a_pass, 7, 1, 1,), (a_pass, 7, 0, 2,), (a_pass, 7, 1, 2,), (y_pass, 8, 0, 0,), (y_pass, 8, 1, 0,), (y_pass, 8, 0, 1,), (y_pass, 8, 1, 1,), (a_pass, 8, 0, 0,), (a_pass, 8, 1, 0,), (a_pass, 8, 0, 1,), (a_pass, 8, 1, 1,), (a_pass, 8, 0, 2,), (a_pass, 8, 1, 2,), (y_pass, 9, 0, 0,), (y_pass, 9, 1, 0,), (y_pass, 9, 0, 1,), (y_pass, 9, 1, 1,), (a_turn, 5, 0,), (a_turn, 5, 1,), (a_turn, 5, 2,), (a_pass, 9, 0, 0,), (a_pass, 9, 1, 0,), (a_pass, 9, 0, 1,), (a_pass, 9, 1, 1,), (a_pass, 9, 0, 2,), (a_pass, 9, 1, 2,), (y_pass, 10, 0, 0,), (y_pass, 10, 1, 0,), (y_pass, 10, 0, 1,), (y_pass, 10, 1, 1,), (a_pass, 10, 0, 0,), (a_pass, 10, 1, 0,), (a_pass, 10, 0, 1,), (a_pass, 10, 1, 1,), (a_pass, 10, 0, 2,), (a_pass, 10, 1, 2,), (y_pass, 11, 0, 0,), (y_pass, 11, 0, 1,), (a_pass, 11, 0, 0,), (a_pass, 11, 0, 1,), (a_pass, 11, 0, 2,), (y_pass, 11, 1, 0,), (y_pass, 11, 1, 1,), (a_pass, 11, 1, 0,), (a_pass, 11, 1, 1,), (a_pass, 11, 1, 2,)],
+                [(left_out, 0, 0,), (left_out, 0, 1,), (right_interleave, 1, 0,), (x_out, 0, 0,), (x_out, 0, 1,), (left_out, 1, 0,), (left_out, 1, 1,), (x_out, 0, 2,), (x_out, 0, 3,), (x_out, 1, 0,), (x_out, 1, 1,), (x_out, 1, 2,), (left_out, 2, 0,), (left_out, 2, 1,), (x_out, 1, 3,), (x_out, 2, 0,), (y_out, 0, 0,), (y_out, 0, 1,), (x_out, 2, 1,), (x_out, 2, 2,), (a_reorder, 0,), (x_out, 2, 3,), (y_out, 1, 0,), (y_out, 1, 1,), (x_out, 3, 0,), (x_out, 3, 1,), (x_out, 3, 2,), (a_reorder, 1,), (x_out, 3, 3,), (x_out, 4, 0,), (x_out, 4, 1,), (x_out, 4, 2,), (a_out, 0, 0,), (a_out, 0, 1,), (a_out, 0, 2,), (a_reorder, 2,), (x_out, 4, 3,), (y_out, 2, 0,), (y_out, 2, 1,), (x_out, 5, 0,), (x_out, 5, 1,), (a_reorder, 3,), (x_out, 5, 2,), (x_out, 5, 3,), (a_out, 1, 0,), (a_out, 1, 1,), (a_out, 1, 2,), (y_out, 3, 0,), (y_out, 3, 1,), (y_out, 4, 0,), (y_out, 4, 1,), (a_reorder, 4,), (a_reorder, 5,), (a_out, 2, 0,), (a_out, 2, 1,), (a_out, 2, 2,), (y_out, 5, 0,), (y_out, 5, 1,), (a_reorder, 6,), (a_reorder, 7,), (a_out, 3, 0,), (a_out, 3, 1,), (a_out, 3, 2,), (a_reorder, 8,), (a_reorder, 9,), (a_out, 4, 0,), (a_out, 4, 1,), (a_out, 4, 2,), (a_reorder, 10,), (a_reorder, 11,), (a_out, 5, 0,), (a_out, 5, 1,), (a_out, 5, 2,)],
+                [(right_interleave, 0, 0,), (left_quantize, 0, 0,), (right_quantize, 0, 0,), (left_quantize, 0, 1,), (right_interleave, 0, 1,), (right_quantize, 0, 1,), (clear_b_scales,), (right_interleave, 1, 1,), (right_quantize, 1, 0,), (right_quantize, 1, 1,), (y_multiply, 0, 0,), (y_multiply, 0, 1,), (y_multiply, 0, 2,), (y_multiply, 0, 3,), (left_quantize, 1, 0,), (left_quantize, 1, 1,), (y_multiply, 1, 0,), (y_multiply, 1, 1,), (y_multiply, 1, 2,), (x_quantize, 0,), (left_quantize, 2, 0,), (left_quantize, 2, 1,), (y_multiply, 1, 3,), (x_quantize, 1,), (a_multiply, 0,), (y_multiply, 2, 0,), (y_multiply, 2, 1,), (y_quantize, 0, 0,), (y_quantize, 0, 1,), (y_multiply, 2, 2,), (a_multiply, 1,), (y_multiply, 2, 3,), (y_quantize, 1, 0,), (y_quantize, 1, 1,), (y_multiply, 3, 0,), (y_multiply, 3, 1,), (x_quantize, 2,), (y_multiply, 3, 2,), (y_multiply, 3, 3,), (a_multiply, 2,), (y_multiply, 4, 0,), (y_multiply, 4, 1,), (x_quantize, 3,), (a_quantize, 0, 0,), (a_quantize, 0, 1,), (a_quantize, 0, 2,), (y_multiply, 4, 2,), (y_multiply, 4, 3,), (a_multiply, 3,), (y_multiply, 5, 0,), (y_multiply, 5, 1,), (x_quantize, 4,), (y_multiply, 5, 2,), (y_multiply, 5, 3,), (x_quantize, 5,), (a_quantize, 1, 0,), (a_quantize, 1, 1,), (a_quantize, 1, 2,), (y_quantize, 2, 0,), (y_quantize, 2, 1,), (a_multiply, 4,), (y_quantize, 3, 0,), (y_quantize, 3, 1,), (a_multiply, 5,), (subtract_c, 0, 0,), (subtract_c, 0, 1,), (subtract_c, 1, 0,), (subtract_c, 1, 1,), (subtract_c, 2, 0,), (subtract_c, 2, 1,), (a_multiply, 6,), (y_quantize, 4, 0,), (y_quantize, 4, 1,), (a_quantize, 2, 0,), (a_quantize, 2, 1,), (a_quantize, 2, 2,), (y_quantize, 5, 0,), (y_quantize, 5, 1,), (a_multiply, 7,), (subtract_c, 3, 0,), (subtract_c, 3, 1,), (a_multiply, 8,), (a_quantize, 3, 0,), (a_quantize, 3, 1,), (a_quantize, 3, 2,), (a_multiply, 9,), (subtract_c, 4, 0,), (subtract_c, 4, 1,), (subtract_c, 5, 0,), (subtract_c, 5, 1,), (a_multiply, 10,), (a_quantize, 4, 0,), (a_quantize, 4, 1,), (a_quantize, 4, 2,), (a_multiply, 11,), (subtract_c, 6, 0,), (subtract_c, 6, 1,), (subtract_c, 7, 0,), (subtract_c, 7, 1,), (a_quantize, 5, 0,), (a_quantize, 5, 1,), (a_quantize, 5, 2,), (subtract_c, 8, 0,), (subtract_c, 8, 1,), (subtract_c, 9, 0,), (subtract_c, 9, 1,), (subtract_c, 10, 0,), (subtract_c, 10, 1,), (subtract_c, 11, 0,), (subtract_c, 11, 1,)],
+            ))

@@ -66,9 +66,10 @@ def tile_sylvester_scaled_residual_s8_kernel(
             free_banks.append(bank_of[key])
 
         def work_tile(key, shape, dtype, name, bufs):
-            new = work.tile(shape, dtype, name=name, bufs=bufs, align_bytes=64)
-            tiles[key] = new
-            return new
+            if key not in tiles:
+                new = work.tile(shape, dtype, name=name, bufs=bufs, align_bytes=64)
+                tiles[key] = new
+            return tiles[key]
 
         def quantize(codes, scales, src):
             nc.vector.quantize_mx(
@@ -80,7 +81,7 @@ def tile_sylvester_scaled_residual_s8_kernel(
 
         def copy_words(dst, ps):
             nc.scalar.copy(
-                out=dst[:].rearrange("p c t -> p (c t)").bitcast(F32).rearrange("p (w r u) -> p w r u", w=2, u=2),
+                out=dst.rearrange("p c t -> p (c t)").bitcast(F32).rearrange("p (w r u) -> p w r u", w=2, u=2),
                 in_=ps[:].rearrange("p (w u r) -> p w r u", w=2, u=2),
             )
 
@@ -88,8 +89,7 @@ def tile_sylvester_scaled_residual_s8_kernel(
             return src[512 * g : 512 * g + 512, :].rearrange("(p t) n -> p t n", t=4)
 
         def load_left(g, lo, hi):
-            if lo == 0:
-                work_tile(("left", g), [P, 4, K], BF16, "left_rows", 3)
+            work_tile(("left", g), [P, 4, K], BF16, "left_rows", 3)
             nc.sync.dma_start(out=tiles["left", g][:, lo:hi, :], in_=rows_view(left, g)[:, lo:hi, :])
 
         def load_right(h):
@@ -98,9 +98,9 @@ def tile_sylvester_scaled_residual_s8_kernel(
                 out=rows[:], in_=right.rearrange("(p t) n -> p t n", t=4)[:, :, 512 * h : 512 * h + 512]
             )
 
-        def load_d(g):
-            rows = work_tile(("d", g), [P, 4, N], BF16, "field_rows", 4)
-            nc.sync.dma_start(out=rows[:], in_=rows_view(d, g))
+        def load_d(g, h):
+            rows = work_tile(("d", g), [P, HALVES, 4, 512], BF16, "field_rows", 4)
+            nc.sync.dma_start(out=rows[:, h], in_=rows_view(d, g)[:, :, 512 * h : 512 * h + 512])
 
         def load_c(g):
             rows = work_tile(("c", g), [P, 4, N], BF16, "field_rows", 4)
@@ -137,7 +137,7 @@ def tile_sylvester_scaled_residual_s8_kernel(
                     turn(ps, (2 * tt + u) * P, words[:, u : K // 2 : 2])
 
         def left_out(g, tp):
-            copy_words(work_tile(("left_t", g, tp), [P, 256, 4], BF16, "left_t", 2), banks["left", g, tp])
+            copy_words(work_tile(("left_t", g, tp), [P, 256, 4], BF16, "left_t", 2)[:], banks["left", g, tp])
             drop_bank(("left", g, tp))
 
         def left_quantize(g, tp):
@@ -180,8 +180,7 @@ def tile_sylvester_scaled_residual_s8_kernel(
                 )
 
         def x_out(j, s):
-            if s == 0:
-                work_tile(("x_t", j), [P, 512, 4], BF16, "x_t", 2)
+            work_tile(("x_t", j), [P, 512, 4], BF16, "x_t", 4)
             u, half = s // 2, s % 2
             nc.scalar.copy(
                 out=tiles["x_t", j][:].rearrange("p (q u e) t -> p u q e t", u=2, e=2)[:, u, 64 * half : 64 * half + 64],
@@ -194,14 +193,13 @@ def tile_sylvester_scaled_residual_s8_kernel(
             quantize(x_codes[:, g, cols], x_scales[:, g, cols], tiles["x_t", j])
 
         def y_multiply(j, s):
-            if s == 0:
-                work_tile(("y_rows", j), [P, 4, 2, 256], BF16, "y_rows", 3)
+            work_tile(("y_rows", j), [P, 4, 2, 256], BF16, "y_rows", 3)
             g, h = j // 2, j % 2
             u, half = s // 2, s % 2
             nc.vector.tensor_tensor(
                 out=tiles["y_rows", j][:, :, u, P * half : P * half + P].rearrange("p t (q e) -> p t q e", e=2),
                 in0=banks["x", j, s][:].rearrange("p (t q e) -> p t q e", t=4, e=2),
-                in1=tiles["d", g][:, :, 512 * h : 512 * h + 512].rearrange("p t (q u e) -> p u t q e", u=2, e=2)[
+                in1=tiles["d", g][:, h].rearrange("p t (q u e) -> p u t q e", u=2, e=2)[
                     :, u, :, 64 * half : 64 * half + 64
                 ],
                 op=MULT,
@@ -215,13 +213,13 @@ def tile_sylvester_scaled_residual_s8_kernel(
                     turn(ps, (2 * tt + u) * P, tiles["y_rows", j][:, 2 * tp + tt, u, :].bitcast(F32))
 
         def y_out(j, tp):
-            copy_words(work_tile(("y_t", j, tp), [P, 256, 4], BF16, "y_t", 4), banks["y", j, tp])
+            work_tile(("y_t", j), [P, 512, 4], BF16, "y_t", 2)
+            copy_words(tiles["y_t", j][:, 256 * tp : 256 * tp + 256, :], banks["y", j, tp])
             drop_bank(("y", j, tp))
 
-        def y_quantize(j, tp):
-            g, h = j // 2, j % 2
-            at = 512 * g + 256 * tp
-            quantize(y_codes[:, h, at : at + 256], y_scales[:, h, at : at + 256], tiles["y_t", j, tp])
+        def y_quantize(j):
+            h, cols = j % 2, slice(512 * (j // 2), 512 * (j // 2) + 512)
+            quantize(y_codes[:, h, cols], y_scales[:, h, cols], tiles["y_t", j])
 
         def a_multiply(i):
             vals = work_tile(("a_values", i), [P, M], BF16, "a_values", 2)
@@ -242,55 +240,73 @@ def tile_sylvester_scaled_residual_s8_kernel(
                     turn(ps, (2 * tt + u) * P, tiles["a_words", 2 * pair + tt][:, g, u, :])
 
         def a_out(pair, g):
-            copy_words(work_tile(("a_t", pair, g), [P, 256, 4], BF16, "a_t", 4), banks["a", pair, g])
+            copy_words(work_tile(("a_t", pair, g), [P, 256, 4], BF16, "a_t", 4)[:], banks["a", pair, g])
             drop_bank(("a", pair, g))
 
         def a_quantize(pair, g):
             cols = slice(256 * pair, 256 * pair + 256)
             quantize(a_codes[:, g, cols], a_scales[:, g, cols], tiles["a_t", pair, g])
 
-        passes = {}
-
-        def open_pass(i, n):
-            passes[i, n] = passes.get((i, n), 0) + 1
-            if passes[i, n] == 1:
-                take_bank(("out", i, n))
-            return dict(
-                out=banks["out", i, n][:], start=(passes[i, n] == 1), stop=(passes[i, n] == HALVES + GROUPS)
-            )
-
-        def y_pass(i, n, h):
+        def y_pass(i, n0, h, out, width, **flags):
             rows = slice(P * i, P * i + P)
             nc.tensor.matmul_mx(
+                out=out,
                 lhsT=y_codes[:, h, rows].bitcast(FP8X4),
                 lhsT_scale=y_scales[:, h, rows],
-                rhs=words_b[:, h, 1024 * n : 1024 * n + 1024].bitcast(FP4X4),
-                rhs_scale=scales_b[:, h, 512 * n : 512 * n + 512],
-                **open_pass(i, n),
+                rhs=words_b[:, h, 2 * n0 : 2 * n0 + 2 * width].bitcast(FP4X4),
+                rhs_scale=scales_b[:, h, n0 : n0 + width],
+                **flags,
             )
 
-        def a_pass(i, n, g):
+        def a_pass(i, n0, g, out, width, **flags):
             rows = slice(P * i, P * i + P)
-            cols = slice(512 * n, 512 * n + 512)
             nc.tensor.matmul_mx(
+                out=out,
                 lhsT=a_codes[:, g, rows].bitcast(FP8X4),
                 lhsT_scale=a_scales[:, g, rows],
-                rhs=x_codes[:, g, cols].bitcast(FP8X4),
-                rhs_scale=x_scales[:, g, cols],
-                **open_pass(i, n),
+                rhs=x_codes[:, g, n0 : n0 + width].bitcast(FP8X4),
+                rhs_scale=x_scales[:, g, n0 : n0 + width],
+                **flags,
             )
 
-        def subtract_c(i, n):
-            if n == 0:
-                work_tile(("result", i), [P, N], F32, "result", 4)
-            cols = slice(512 * n, 512 * n + 512)
+        passes = {}
+
+        def wide_flags(i, n0):
+            passes[i, n0] = passes.get((i, n0), 0) + 1
+            if passes[i, n0] == 1:
+                take_bank(("out", i, n0))
+            return dict(
+                out=banks["out", i, n0][:],
+                width=512,
+                start=(passes[i, n0] == 1),
+                stop=(passes[i, n0] == HALVES + GROUPS),
+            )
+
+        def wide_y(i, n0, h):
+            y_pass(i, n0, h, **wide_flags(i, n0))
+
+        def wide_a(i, n0, g):
+            a_pass(i, n0, g, **wide_flags(i, n0))
+
+        def narrow(i, n0):
+            if n0 % 256 == 0:
+                take_bank(("out", i, n0))
+            at = n0 % 256
+            ps = banks["out", i, n0 - at][:, at : at + P]
+            for h in range(HALVES):
+                y_pass(i, n0, h, ps, P, start=(h == 0), stop=False)
+            for g in range(GROUPS):
+                a_pass(i, n0, g, ps, P, start=False, stop=(g == GROUPS - 1))
+
+        def subtract_c(i, n0, n1):
+            work_tile(("result", i), [P, N], F32, "result", 4)
             nc.vector.tensor_tensor(
-                out=tiles["result", i][:, cols],
-                in0=banks["out", i, n][:],
-                in1=tiles["c", i // 4][:, i % 4, cols],
+                out=tiles["result", i][:, n0:n1],
+                in0=banks["out", i, n0][:, : n1 - n0],
+                in1=tiles["c", i // 4][:, i % 4, n0:n1],
                 op=SUB,
             )
-            drop_bank(("out", i, n))
+            drop_bank(("out", i, n0))
 
         def needs(step):
             f, x = step[0], step[1:]
@@ -308,17 +324,17 @@ def tile_sylvester_scaled_residual_s8_kernel(
             if f == x_matmul:
                 return [(left_quantize, x[0] // 2, tp) for tp in range(2)] + [(right_quantize, x[0] % 2, x[1] // 2)]
             if f == x_out:
-                return [(x_matmul,) + x] + ([(x_quantize, x[0] - 2)] if x[0] > 1 else [])
+                return [(x_matmul,) + x] + ([(x_quantize, x[0] - 4)] if x[0] > 3 else [])
             if f == y_multiply:
-                return [(x_matmul,) + x, (load_d, x[0] // 2)] + ([(y_turn, x[0] - 3, 1)] if x[0] > 2 else [])
+                return [(x_matmul,) + x, (load_d, x[0] // 2, x[0] % 2)] + ([(y_turn, x[0] - 3, 1)] if x[0] > 2 else [])
             if f == x_quantize:
                 return [(x_out, x[0], s) for s in range(4)]
             if f == y_turn:
                 return [(y_multiply, x[0], s) for s in range(4)]
             if f == y_out:
-                return [(y_turn,) + x] + ([(y_quantize, x[0] - 2, x[1])] if x[0] > 1 else [])
+                return [(y_turn,) + x] + ([(y_quantize, x[0] - 2)] if x[0] > 1 else [])
             if f == y_quantize:
-                return [(y_out,) + x]
+                return [(y_out, x[0], tp) for tp in range(2)]
             if f == a_multiply:
                 return [(load_a_scale,), (load_a, x[0] // 2)] + ([(a_reorder, x[0] - 2)] if x[0] > 1 else [])
             if f == a_reorder:
@@ -330,23 +346,25 @@ def tile_sylvester_scaled_residual_s8_kernel(
                 return [(a_turn,) + x] + ([(a_quantize, n // 3, n % 3)] if n >= 0 else [])
             if f == a_quantize:
                 return [(a_out,) + x]
-            if f == y_pass:
-                return [(y_quantize, 2 * (x[0] // 4) + x[2], x[0] % 4 // 2), (load_b,)]
-            if f == a_pass:
-                return [(a_quantize, x[0] // 2, x[2]), (x_quantize, 2 * x[2] + x[1])]
+            if f == wide_y:
+                return [(y_quantize, 2 * (x[0] // 4) + x[2]), (load_b,)]
+            if f == wide_a:
+                return [(a_quantize, x[0] // 2, x[2]), (x_quantize, 2 * x[2] + x[1] // 512)]
+            if f == narrow:
+                return [(a_quantize, x[0] // 2, GROUPS - 1), (y_quantize, 2 * GROUPS - 1)]
             if f == subtract_c:
-                return (
-                    [(y_pass,) + x + (h,) for h in range(HALVES)]
-                    + [(a_pass,) + x + (g,) for g in range(GROUPS)]
-                    + [(load_c, x[0] // 4)]
-                    + ([(store, x[0] - 4, 0, N)] if x[0] > 3 else [])
-                )
+                i, n0, n1 = x
+                made = [(narrow, i, n0), (narrow, i, n0 + P)]
+                if n1 - n0 == 512:
+                    made = [(wide_y, i, n0, h) for h in range(HALVES)] + [(wide_a, i, n0, g) for g in range(GROUPS)]
+                return made + [(load_c, i // 4)] + ([(store, i - 4, 0, N)] if i > 3 else [])
             if f == store:
-                return [(subtract_c, x[0], n) for n in range(x[1] // 512, x[2] // 512)]
+                i, n0, n1 = x
+                return [(subtract_c, i, 0, 512), (subtract_c, i, 512, N)] if n1 - n0 == N else [(subtract_c,) + x]
             if f == load_b:
                 return [(clear_b_scales,)]
             if f == load_c and x[0] > 0:
-                return [(y_multiply, 2 * x[0] - 1, 3)]
+                return [(y_multiply, 2 * x[0] - 2 + h, s) for h in range(HALVES) for s in range(4)]
             return []
 
         TAKES_BANK = (left_turn, x_matmul, y_turn, a_turn)
@@ -361,20 +379,24 @@ def tile_sylvester_scaled_residual_s8_kernel(
                         continue
                     step = q[0]
                     f, x = step[0], step[1:]
-                    opens = f in TAKES_BANK or (f in (y_pass, a_pass) and x[:2] not in passes)
+                    opens = (
+                        f in TAKES_BANK
+                        or (f in (wide_y, wide_a) and x[:2] not in passes)
+                        or (f == narrow and x[1] % 256 == 0)
+                    )
                     if (opens and not free_banks) or any(s not in issued for s in needs(step)):
                         continue
                     f(*x)
                     issued.add(step)
                     q.pop(0)
                     stuck = False
-                assert not stuck
+                assert not stuck, [q[0] for q in left_over if q]
 
         make_identity(nc, ident[:])
         with tc.manual_schedule():
             issue((
-                [(load_left, 0, 0, 2), (load_left, 0, 2, 4), (load_right, 0), (load_right, 1), (load_left, 1, 0, 4), (load_d, 0), (load_left, 2, 0, 4), (load_a_scale,), (load_a, 0), (load_d, 1), (load_a, 1), (load_d, 2), (load_b,), (load_a, 2), (load_c, 0), (load_c, 1), (load_a, 3), (load_a, 4), (load_a, 5), (load_c, 2), (store, 0, 0, N), (store, 1, 0, N), (store, 2, 0, N), (store, 3, 0, N), (store, 4, 0, N), (store, 5, 0, N), (store, 6, 0, N), (store, 7, 0, N), (store, 8, 0, N), (store, 9, 0, N), (store, 10, 0, N), (store, 11, 0, 512), (store, 11, 512, 1024)],
-                [(left_turn, 0, 0,), (left_turn, 0, 1,), (x_matmul, 0, 0,), (x_matmul, 0, 1,), (left_turn, 1, 0,), (left_turn, 1, 1,), (x_matmul, 0, 2,), (x_matmul, 0, 3,), (x_matmul, 1, 0,), (x_matmul, 1, 1,), (x_matmul, 1, 2,), (x_matmul, 1, 3,), (left_turn, 2, 0,), (left_turn, 2, 1,), (y_turn, 0, 0,), (y_turn, 0, 1,), (x_matmul, 2, 0,), (x_matmul, 2, 1,), (x_matmul, 2, 2,), (x_matmul, 2, 3,), (y_turn, 1, 0,), (y_turn, 1, 1,), (x_matmul, 3, 0,), (x_matmul, 3, 1,), (x_matmul, 3, 2,), (x_matmul, 3, 3,), (x_matmul, 4, 0,), (x_matmul, 4, 1,), (x_matmul, 4, 2,), (x_matmul, 4, 3,), (a_turn, 0, 0,), (a_turn, 0, 1,), (a_turn, 0, 2,), (y_turn, 2, 0,), (y_turn, 2, 1,), (y_pass, 0, 0, 0,), (y_pass, 0, 1, 0,), (y_pass, 0, 0, 1,), (y_pass, 0, 1, 1,), (x_matmul, 5, 0,), (x_matmul, 5, 1,), (x_matmul, 5, 2,), (x_matmul, 5, 3,), (y_pass, 1, 0, 0,), (y_pass, 1, 1, 0,), (y_pass, 1, 0, 1,), (y_pass, 1, 1, 1,), (a_pass, 0, 0, 0,), (a_pass, 0, 1, 0,), (a_pass, 0, 0, 1,), (a_pass, 0, 1, 1,), (a_pass, 1, 0, 0,), (a_pass, 1, 1, 0,), (a_turn, 1, 0,), (a_turn, 1, 1,), (a_turn, 1, 2,), (y_turn, 3, 0,), (y_turn, 3, 1,), (y_turn, 4, 0,), (y_turn, 4, 1,), (a_pass, 0, 0, 2,), (a_pass, 0, 1, 2,), (a_pass, 1, 0, 1,), (a_pass, 1, 1, 1,), (a_pass, 1, 0, 2,), (a_pass, 1, 1, 2,), (y_pass, 2, 0, 0,), (y_pass, 2, 1, 0,), (y_pass, 2, 0, 1,), (y_pass, 2, 1, 1,), (a_pass, 2, 0, 0,), (a_pass, 2, 1, 0,), (a_pass, 2, 0, 1,), (a_pass, 2, 1, 1,), (a_pass, 2, 0, 2,), (a_pass, 2, 1, 2,), (y_pass, 3, 0, 0,), (y_pass, 3, 1, 0,), (y_pass, 3, 0, 1,), (y_pass, 3, 1, 1,), (a_turn, 2, 0,), (a_turn, 2, 1,), (a_turn, 2, 2,), (y_turn, 5, 0,), (y_turn, 5, 1,), (a_pass, 3, 0, 0,), (a_pass, 3, 1, 0,), (a_pass, 3, 0, 1,), (a_pass, 3, 1, 1,), (a_pass, 3, 0, 2,), (a_pass, 3, 1, 2,), (y_pass, 4, 0, 0,), (y_pass, 4, 1, 0,), (y_pass, 4, 0, 1,), (y_pass, 4, 1, 1,), (a_pass, 4, 0, 0,), (a_pass, 4, 1, 0,), (a_pass, 4, 0, 1,), (a_pass, 4, 1, 1,), (a_pass, 4, 0, 2,), (a_pass, 4, 1, 2,), (y_pass, 5, 0, 0,), (y_pass, 5, 1, 0,), (y_pass, 5, 0, 1,), (y_pass, 5, 1, 1,), (a_turn, 3, 0,), (a_turn, 3, 1,), (a_turn, 3, 2,), (a_pass, 5, 0, 0,), (a_pass, 5, 1, 0,), (a_pass, 5, 0, 1,), (a_pass, 5, 1, 1,), (a_pass, 5, 0, 2,), (a_pass, 5, 1, 2,), (y_pass, 6, 0, 0,), (y_pass, 6, 1, 0,), (y_pass, 6, 0, 1,), (y_pass, 6, 1, 1,), (a_pass, 6, 0, 0,), (a_pass, 6, 1, 0,), (a_pass, 6, 0, 1,), (a_pass, 6, 1, 1,), (a_pass, 6, 0, 2,), (a_pass, 6, 1, 2,), (y_pass, 7, 0, 0,), (y_pass, 7, 1, 0,), (y_pass, 7, 0, 1,), (y_pass, 7, 1, 1,), (a_turn, 4, 0,), (a_turn, 4, 1,), (a_turn, 4, 2,), (a_pass, 7, 0, 0,), (a_pass, 7, 1, 0,), (a_pass, 7, 0, 1,), (a_pass, 7, 1, 1,), (a_pass, 7, 0, 2,), (a_pass, 7, 1, 2,), (y_pass, 8, 0, 0,), (y_pass, 8, 1, 0,), (y_pass, 8, 0, 1,), (y_pass, 8, 1, 1,), (a_pass, 8, 0, 0,), (a_pass, 8, 1, 0,), (a_pass, 8, 0, 1,), (a_pass, 8, 1, 1,), (a_pass, 8, 0, 2,), (a_pass, 8, 1, 2,), (y_pass, 9, 0, 0,), (y_pass, 9, 1, 0,), (y_pass, 9, 0, 1,), (y_pass, 9, 1, 1,), (a_turn, 5, 0,), (a_turn, 5, 1,), (a_turn, 5, 2,), (a_pass, 9, 0, 0,), (a_pass, 9, 1, 0,), (a_pass, 9, 0, 1,), (a_pass, 9, 1, 1,), (a_pass, 9, 0, 2,), (a_pass, 9, 1, 2,), (y_pass, 10, 0, 0,), (y_pass, 10, 1, 0,), (y_pass, 10, 0, 1,), (y_pass, 10, 1, 1,), (a_pass, 10, 0, 0,), (a_pass, 10, 1, 0,), (a_pass, 10, 0, 1,), (a_pass, 10, 1, 1,), (a_pass, 10, 0, 2,), (a_pass, 10, 1, 2,), (y_pass, 11, 0, 0,), (y_pass, 11, 0, 1,), (a_pass, 11, 0, 0,), (a_pass, 11, 0, 1,), (a_pass, 11, 0, 2,), (y_pass, 11, 1, 0,), (y_pass, 11, 1, 1,), (a_pass, 11, 1, 0,), (a_pass, 11, 1, 1,), (a_pass, 11, 1, 2,)],
-                [(left_out, 0, 0,), (left_out, 0, 1,), (right_interleave, 1, 0,), (x_out, 0, 0,), (x_out, 0, 1,), (left_out, 1, 0,), (left_out, 1, 1,), (x_out, 0, 2,), (x_out, 0, 3,), (x_out, 1, 0,), (x_out, 1, 1,), (x_out, 1, 2,), (left_out, 2, 0,), (left_out, 2, 1,), (x_out, 1, 3,), (x_out, 2, 0,), (y_out, 0, 0,), (y_out, 0, 1,), (x_out, 2, 1,), (x_out, 2, 2,), (a_reorder, 0,), (x_out, 2, 3,), (y_out, 1, 0,), (y_out, 1, 1,), (x_out, 3, 0,), (x_out, 3, 1,), (x_out, 3, 2,), (a_reorder, 1,), (x_out, 3, 3,), (x_out, 4, 0,), (x_out, 4, 1,), (x_out, 4, 2,), (a_out, 0, 0,), (a_out, 0, 1,), (a_out, 0, 2,), (a_reorder, 2,), (x_out, 4, 3,), (y_out, 2, 0,), (y_out, 2, 1,), (x_out, 5, 0,), (x_out, 5, 1,), (a_reorder, 3,), (x_out, 5, 2,), (x_out, 5, 3,), (a_out, 1, 0,), (a_out, 1, 1,), (a_out, 1, 2,), (y_out, 3, 0,), (y_out, 3, 1,), (y_out, 4, 0,), (y_out, 4, 1,), (a_reorder, 4,), (a_reorder, 5,), (a_out, 2, 0,), (a_out, 2, 1,), (a_out, 2, 2,), (y_out, 5, 0,), (y_out, 5, 1,), (a_reorder, 6,), (a_reorder, 7,), (a_out, 3, 0,), (a_out, 3, 1,), (a_out, 3, 2,), (a_reorder, 8,), (a_reorder, 9,), (a_out, 4, 0,), (a_out, 4, 1,), (a_out, 4, 2,), (a_reorder, 10,), (a_reorder, 11,), (a_out, 5, 0,), (a_out, 5, 1,), (a_out, 5, 2,)],
-                [(right_interleave, 0, 0,), (left_quantize, 0, 0,), (right_quantize, 0, 0,), (left_quantize, 0, 1,), (right_interleave, 0, 1,), (right_quantize, 0, 1,), (clear_b_scales,), (right_interleave, 1, 1,), (right_quantize, 1, 0,), (right_quantize, 1, 1,), (y_multiply, 0, 0,), (y_multiply, 0, 1,), (y_multiply, 0, 2,), (y_multiply, 0, 3,), (left_quantize, 1, 0,), (left_quantize, 1, 1,), (y_multiply, 1, 0,), (y_multiply, 1, 1,), (y_multiply, 1, 2,), (x_quantize, 0,), (left_quantize, 2, 0,), (left_quantize, 2, 1,), (y_multiply, 1, 3,), (x_quantize, 1,), (a_multiply, 0,), (y_multiply, 2, 0,), (y_multiply, 2, 1,), (y_quantize, 0, 0,), (y_quantize, 0, 1,), (y_multiply, 2, 2,), (a_multiply, 1,), (y_multiply, 2, 3,), (y_quantize, 1, 0,), (y_quantize, 1, 1,), (y_multiply, 3, 0,), (y_multiply, 3, 1,), (x_quantize, 2,), (y_multiply, 3, 2,), (y_multiply, 3, 3,), (a_multiply, 2,), (y_multiply, 4, 0,), (y_multiply, 4, 1,), (x_quantize, 3,), (a_quantize, 0, 0,), (a_quantize, 0, 1,), (a_quantize, 0, 2,), (y_multiply, 4, 2,), (y_multiply, 4, 3,), (a_multiply, 3,), (y_multiply, 5, 0,), (y_multiply, 5, 1,), (x_quantize, 4,), (y_multiply, 5, 2,), (y_multiply, 5, 3,), (x_quantize, 5,), (a_quantize, 1, 0,), (a_quantize, 1, 1,), (a_quantize, 1, 2,), (y_quantize, 2, 0,), (y_quantize, 2, 1,), (a_multiply, 4,), (y_quantize, 3, 0,), (y_quantize, 3, 1,), (a_multiply, 5,), (subtract_c, 0, 0,), (subtract_c, 0, 1,), (subtract_c, 1, 0,), (subtract_c, 1, 1,), (subtract_c, 2, 0,), (subtract_c, 2, 1,), (a_multiply, 6,), (y_quantize, 4, 0,), (y_quantize, 4, 1,), (a_quantize, 2, 0,), (a_quantize, 2, 1,), (a_quantize, 2, 2,), (y_quantize, 5, 0,), (y_quantize, 5, 1,), (a_multiply, 7,), (subtract_c, 3, 0,), (subtract_c, 3, 1,), (a_multiply, 8,), (a_quantize, 3, 0,), (a_quantize, 3, 1,), (a_quantize, 3, 2,), (a_multiply, 9,), (subtract_c, 4, 0,), (subtract_c, 4, 1,), (subtract_c, 5, 0,), (subtract_c, 5, 1,), (a_multiply, 10,), (a_quantize, 4, 0,), (a_quantize, 4, 1,), (a_quantize, 4, 2,), (a_multiply, 11,), (subtract_c, 6, 0,), (subtract_c, 6, 1,), (subtract_c, 7, 0,), (subtract_c, 7, 1,), (a_quantize, 5, 0,), (a_quantize, 5, 1,), (a_quantize, 5, 2,), (subtract_c, 8, 0,), (subtract_c, 8, 1,), (subtract_c, 9, 0,), (subtract_c, 9, 1,), (subtract_c, 10, 0,), (subtract_c, 10, 1,), (subtract_c, 11, 0,), (subtract_c, 11, 1,)],
+                [(load_left, 0, 0, 2), (load_left, 0, 2, 4), (load_right, 0), (load_right, 1), (load_left, 1, 0, 4), (load_d, 0, 0), (load_d, 0, 1), (load_left, 2, 0, 4), (load_a_scale,), (load_a, 0), (load_d, 1, 0), (load_d, 1, 1), (load_a, 1), (load_b,), (load_a, 2), (load_d, 2, 0), (load_d, 2, 1), (load_c, 0), (load_c, 1), (load_a, 3), (load_a, 4), (load_c, 2), (load_a, 5), (store, 0, 0, N), (store, 1, 0, N), (store, 2, 0, N), (store, 3, 0, N), (store, 4, 0, N), (store, 5, 0, N), (store, 6, 0, N), (store, 7, 0, N), (store, 8, 0, N), (store, 9, 0, N), (store, 10, 0, N), (store, 11, 0, 512), (store, 11, 512, 768), (store, 11, 768, 1024)],
+                [(left_turn, 0, 0,), (left_turn, 0, 1,), (x_matmul, 0, 0,), (x_matmul, 0, 1,), (left_turn, 1, 0,), (left_turn, 1, 1,), (x_matmul, 1, 0,), (x_matmul, 1, 1,), (x_matmul, 1, 2,), (x_matmul, 1, 3,), (x_matmul, 0, 2,), (x_matmul, 0, 3,), (left_turn, 2, 0,), (left_turn, 2, 1,), (y_turn, 0, 0,), (y_turn, 0, 1,), (x_matmul, 2, 0,), (x_matmul, 2, 1,), (x_matmul, 2, 2,), (x_matmul, 2, 3,), (x_matmul, 3, 0,), (x_matmul, 3, 1,), (x_matmul, 3, 2,), (x_matmul, 3, 3,), (y_turn, 1, 0,), (y_turn, 1, 1,), (x_matmul, 4, 0,), (x_matmul, 4, 1,), (a_turn, 0, 0,), (a_turn, 0, 1,), (a_turn, 0, 2,), (x_matmul, 4, 2,), (x_matmul, 4, 3,), (y_turn, 2, 0,), (y_turn, 2, 1,), (x_matmul, 5, 0,), (x_matmul, 5, 1,), (wide_y, 0, 0, 0), (wide_y, 0, 512, 0), (wide_y, 0, 0, 1), (wide_y, 0, 512, 1), (x_matmul, 5, 2,), (x_matmul, 5, 3,), (wide_a, 0, 0, 0), (wide_a, 0, 512, 0), (wide_a, 0, 0, 1), (wide_a, 0, 512, 1), (wide_y, 1, 0, 0), (wide_y, 1, 512, 0), (wide_y, 1, 0, 1), (wide_y, 1, 512, 1), (wide_a, 1, 0, 0), (wide_a, 1, 512, 0), (a_turn, 1, 0,), (a_turn, 1, 1,), (a_turn, 1, 2,), (wide_a, 1, 0, 1), (wide_a, 1, 512, 1), (y_turn, 3, 0,), (y_turn, 3, 1,), (y_turn, 4, 0,), (y_turn, 4, 1,), (wide_a, 0, 0, 2), (wide_a, 0, 512, 2), (wide_y, 2, 0, 0), (wide_y, 2, 512, 0), (wide_y, 2, 0, 1), (wide_y, 2, 512, 1), (wide_a, 1, 0, 2), (wide_a, 1, 512, 2), (wide_a, 2, 0, 0), (wide_a, 2, 512, 0), (wide_a, 2, 0, 1), (wide_a, 2, 512, 1), (wide_a, 2, 0, 2), (wide_a, 2, 512, 2), (y_turn, 5, 0,), (y_turn, 5, 1,), (a_turn, 2, 0,), (a_turn, 2, 1,), (a_turn, 2, 2,), (wide_y, 3, 0, 0), (wide_y, 3, 512, 0), (wide_y, 3, 0, 1), (wide_y, 3, 512, 1), (wide_a, 3, 0, 0), (wide_a, 3, 512, 0), (wide_a, 3, 0, 1), (wide_a, 3, 512, 1), (wide_a, 3, 0, 2), (wide_a, 3, 512, 2), (wide_y, 4, 0, 0), (wide_y, 4, 512, 0), (wide_y, 4, 0, 1), (wide_y, 4, 512, 1), (wide_a, 4, 0, 0), (wide_a, 4, 512, 0), (wide_a, 4, 0, 1), (wide_a, 4, 512, 1), (wide_a, 4, 0, 2), (wide_a, 4, 512, 2), (wide_y, 5, 0, 0), (wide_y, 5, 512, 0), (wide_y, 5, 0, 1), (wide_y, 5, 512, 1), (wide_a, 5, 0, 0), (wide_a, 5, 512, 0), (a_turn, 3, 0,), (a_turn, 3, 1,), (a_turn, 3, 2,), (wide_a, 5, 0, 1), (wide_a, 5, 512, 1), (wide_a, 5, 0, 2), (wide_a, 5, 512, 2), (wide_y, 6, 0, 0), (wide_y, 6, 512, 0), (wide_y, 6, 0, 1), (wide_y, 6, 512, 1), (wide_a, 6, 0, 0), (wide_a, 6, 512, 0), (wide_a, 6, 0, 1), (wide_a, 6, 512, 1), (wide_a, 6, 0, 2), (wide_a, 6, 512, 2), (wide_y, 7, 0, 0), (wide_y, 7, 512, 0), (wide_y, 7, 0, 1), (wide_y, 7, 512, 1), (wide_a, 7, 0, 0), (wide_a, 7, 512, 0), (wide_a, 7, 0, 1), (wide_a, 7, 512, 1), (a_turn, 4, 0,), (a_turn, 4, 1,), (a_turn, 4, 2,), (wide_a, 7, 0, 2), (wide_a, 7, 512, 2), (wide_a, 8, 0, 0), (wide_a, 8, 512, 0), (wide_a, 8, 0, 1), (wide_a, 8, 512, 1), (wide_a, 8, 0, 2), (wide_a, 8, 512, 2), (wide_y, 8, 0, 0), (wide_y, 8, 512, 0), (wide_y, 8, 0, 1), (wide_y, 8, 512, 1), (wide_y, 9, 0, 0), (wide_y, 9, 512, 0), (wide_y, 9, 0, 1), (wide_y, 9, 512, 1), (a_turn, 5, 0,), (a_turn, 5, 1,), (a_turn, 5, 2,), (wide_a, 9, 0, 0), (wide_a, 9, 512, 0), (wide_a, 9, 0, 1), (wide_a, 9, 512, 1), (wide_a, 9, 0, 2), (wide_a, 9, 512, 2), (wide_y, 10, 0, 0), (wide_y, 10, 512, 0), (wide_y, 10, 0, 1), (wide_y, 10, 512, 1), (wide_a, 10, 0, 0), (wide_a, 10, 512, 0), (wide_a, 10, 0, 1), (wide_a, 10, 512, 1), (wide_a, 10, 0, 2), (wide_a, 10, 512, 2), (wide_y, 11, 0, 0), (wide_y, 11, 0, 1), (wide_a, 11, 0, 0), (wide_a, 11, 0, 1), (wide_a, 11, 0, 2), (narrow, 11, 512), (narrow, 11, 640), (narrow, 11, 768), (narrow, 11, 896)],
+                [(left_out, 0, 0,), (left_out, 0, 1,), (right_interleave, 1, 0,), (x_out, 0, 0,), (x_out, 0, 1,), (left_out, 1, 0,), (left_out, 1, 1,), (x_out, 0, 2,), (x_out, 0, 3,), (x_out, 1, 0,), (left_out, 2, 0,), (left_out, 2, 1,), (x_out, 1, 1,), (x_out, 1, 2,), (x_out, 1, 3,), (y_out, 0, 0,), (y_out, 0, 1,), (x_out, 2, 1,), (x_out, 2, 2,), (x_out, 2, 3,), (x_out, 2, 0,), (a_reorder, 0,), (x_out, 3, 0,), (x_out, 3, 1,), (x_out, 3, 2,), (y_out, 1, 0,), (y_out, 1, 1,), (a_reorder, 1,), (x_out, 3, 3,), (x_out, 4, 0,), (x_out, 4, 1,), (a_out, 0, 0,), (a_out, 0, 1,), (a_out, 0, 2,), (x_out, 4, 2,), (x_out, 4, 3,), (a_reorder, 2,), (y_out, 2, 0,), (y_out, 2, 1,), (x_out, 5, 0,), (x_out, 5, 1,), (x_out, 5, 2,), (x_out, 5, 3,), (a_reorder, 3,), (a_out, 1, 0,), (a_out, 1, 1,), (a_out, 1, 2,), (y_out, 3, 0,), (y_out, 3, 1,), (y_out, 4, 0,), (y_out, 4, 1,), (a_reorder, 4,), (a_reorder, 5,), (a_out, 2, 0,), (a_out, 2, 1,), (a_out, 2, 2,), (a_reorder, 6,), (y_out, 5, 0,), (y_out, 5, 1,), (a_reorder, 7,), (a_out, 3, 0,), (a_out, 3, 1,), (a_out, 3, 2,), (a_reorder, 8,), (a_reorder, 9,), (a_out, 4, 0,), (a_out, 4, 1,), (a_out, 4, 2,), (a_reorder, 10,), (a_reorder, 11,), (a_out, 5, 0,), (a_out, 5, 1,), (a_out, 5, 2,)],
+                [(clear_b_scales,), (right_interleave, 0, 0,), (left_quantize, 0, 0,), (left_quantize, 0, 1,), (right_quantize, 0, 0,), (right_interleave, 0, 1,), (right_interleave, 1, 1,), (right_quantize, 0, 1,), (right_quantize, 1, 1,), (right_quantize, 1, 0,), (y_multiply, 0, 0,), (y_multiply, 0, 1,), (y_multiply, 1, 0,), (left_quantize, 1, 0,), (left_quantize, 1, 1,), (y_multiply, 1, 3,), (y_multiply, 0, 2,), (y_multiply, 0, 3,), (y_multiply, 1, 1,), (y_multiply, 1, 2,), (left_quantize, 2, 0,), (left_quantize, 2, 1,), (x_quantize, 0,), (a_multiply, 0,), (y_multiply, 2, 0,), (x_quantize, 1,), (y_multiply, 2, 2,), (y_multiply, 2, 1,), (y_quantize, 0), (a_multiply, 1,), (y_multiply, 2, 3,), (y_multiply, 3, 0,), (y_multiply, 3, 1,), (y_multiply, 3, 3,), (y_multiply, 3, 2,), (a_multiply, 2,), (x_quantize, 2,), (y_multiply, 4, 0,), (y_multiply, 4, 1,), (x_quantize, 3,), (y_quantize, 1), (a_quantize, 0, 0,), (a_quantize, 0, 1,), (y_multiply, 4, 2,), (y_multiply, 4, 3,), (a_quantize, 0, 2,), (a_multiply, 3,), (y_multiply, 5, 0,), (y_multiply, 5, 1,), (y_multiply, 5, 2,), (y_multiply, 5, 3,), (x_quantize, 4,), (x_quantize, 5,), (a_quantize, 1, 0,), (a_quantize, 1, 1,), (a_quantize, 1, 2,), (y_quantize, 2), (a_multiply, 4,), (a_multiply, 5,), (subtract_c, 0, 0, 512), (subtract_c, 0, 512, 1024), (subtract_c, 1, 0, 512), (subtract_c, 1, 512, 1024), (y_quantize, 3), (a_multiply, 6,), (a_quantize, 2, 0,), (subtract_c, 2, 0, 512), (subtract_c, 2, 512, 1024), (a_quantize, 2, 1,), (a_quantize, 2, 2,), (y_quantize, 4), (a_multiply, 7,), (y_quantize, 5), (subtract_c, 3, 0, 512), (subtract_c, 3, 512, 1024), (a_multiply, 8,), (a_quantize, 3, 0,), (a_quantize, 3, 1,), (a_quantize, 3, 2,), (a_multiply, 9,), (subtract_c, 4, 0, 512), (subtract_c, 4, 512, 1024), (subtract_c, 5, 0, 512), (subtract_c, 5, 512, 1024), (a_multiply, 10,), (a_quantize, 4, 0,), (a_quantize, 4, 1,), (a_quantize, 4, 2,), (a_multiply, 11,), (subtract_c, 6, 0, 512), (subtract_c, 6, 512, 1024), (subtract_c, 7, 0, 512), (subtract_c, 7, 512, 1024), (a_quantize, 5, 0,), (a_quantize, 5, 1,), (a_quantize, 5, 2,), (subtract_c, 8, 0, 512), (subtract_c, 8, 512, 1024), (subtract_c, 9, 0, 512), (subtract_c, 9, 512, 1024), (subtract_c, 10, 0, 512), (subtract_c, 10, 512, 1024), (subtract_c, 11, 0, 512), (subtract_c, 11, 512, 768), (subtract_c, 11, 768, 1024)],
             ))

@@ -15,12 +15,30 @@ FP8 = mybir.dt.float8_e4m3fn
 FP8X4 = mybir.dt.float8_e4m3fn_x4
 FP4X4 = mybir.dt.float4_e2m1fn_x4
 MULT = mybir.AluOpType.mult
-SUB = mybir.AluOpType.subtract
+SUBTRACT = mybir.AluOpType.subtract
 
 P = 128
-GROUPS = M // 512
-HALVES = N // 512
-TILES = M // P
+PASS = 512
+GROUPS = M // PASS
+HALVES = N // PASS
+BANDS = M // P
+LAST = BANDS - 1
+PSUM_BANKS = 8
+
+DEPTH = {
+    "left_rows": 3,
+    "right_rows": 2,
+    "field_rows": 4,
+    "left_t": 2,
+    "right_t": 4,
+    "x_t": 4,
+    "y_rows": 3,
+    "y_t": 2,
+    "a_values": 2,
+    "a_words": 4,
+    "a_t": 4,
+    "result": 4,
+}
 
 
 def tile_sylvester_scaled_residual_s8_kernel(
@@ -43,134 +61,140 @@ def tile_sylvester_scaled_residual_s8_kernel(
         y_scales = keep.tile([P, HALVES, M], U8, name="y_scales", align_bytes=64)
         a_codes = keep.tile([P, GROUPS, M], U32, name="a_codes", align_bytes=64)
         a_scales = keep.tile([P, GROUPS, M], U8, name="a_scales", align_bytes=64)
-        words_b = keep.tile([P, HALVES, 2 * N], U8, name="words_b", align_bytes=64)
-        scales_b = keep.tile([P, HALVES, N], U8, name="scales_b", align_bytes=64)
-        a_col_scale = keep.tile([P, M], F32, name="a_col_scale", align_bytes=64)
+        b_codes = keep.tile([P, HALVES, 2 * N], U8, name="b_codes", align_bytes=64)
+        b_planes = keep.tile([P, HALVES, N], U8, name="b_planes", align_bytes=64)
+        column_scale = keep.tile([P, M], F32, name="column_scale", align_bytes=64)
         code_bytes = [
             keep.tile([P, 4, M], U8, name="code_bytes%d" % g, align_bytes=64) for g in range(GROUPS)
         ]
 
-        free_banks = list(range(8))
-        banks = {}
-        bank_of = {}
-        tiles = {}
+        held = {}
+        free_banks = list(range(PSUM_BANKS))
+        bank_number = {}
+
+        def rotating(name, key, shape, dtype):
+            if (name, key) not in held:
+                new = work.tile(shape, dtype, name=name, bufs=DEPTH[name], align_bytes=64)
+                held[name, key] = new
+            return held[name, key]
 
         def take_bank(key):
-            b = free_banks.pop(0)
-            bank_of[key] = b
-            ps = psum.tile([P, 512], F32, name="bank%d" % b, tag="bank%d" % b)
-            banks[key] = ps
-            return ps
+            number = free_banks.pop(0)
+            bank_number[key] = number
+            new = psum.tile([P, PASS], F32, name="bank%d" % number, tag="bank%d" % number)
+            held["bank", key] = new
+            return new
 
-        def drop_bank(key):
-            free_banks.append(bank_of[key])
+        def give_back(key):
+            free_banks.append(bank_number[key])
 
-        def work_tile(key, shape, dtype, name, bufs):
-            if key not in tiles:
-                new = work.tile(shape, dtype, name=name, bufs=bufs, align_bytes=64)
-                tiles[key] = new
-            return tiles[key]
+        def band_rows(src, g):
+            return src[PASS * g : PASS * (g + 1), :].rearrange("(p t) n -> p t n", t=4)
 
-        def quantize(codes, scales, src):
-            nc.vector.quantize_mx(
-                out=codes.bitcast(FP8X4), scales=scales, in_=src[:].rearrange("p c t -> p (c t)")
-            )
+        def half(h):
+            return slice(PASS * h, PASS * (h + 1))
 
-        def turn(ps, at, words):
-            nc.tensor.transpose(ps[:, at : at + P], words, ident[:])
+        def transpose(bank, place, words):
+            nc.tensor.transpose(bank[:, P * place : P * (place + 1)], words, ident[:])
 
-        def copy_words(dst, ps):
+        def copy_turned(dst, bank):
             nc.scalar.copy(
-                out=dst.rearrange("p c t -> p (c t)").bitcast(F32).rearrange("p (w r u) -> p w r u", w=2, u=2),
-                in_=ps[:].rearrange("p (w u r) -> p w r u", w=2, u=2),
+                out=dst.rearrange("p c t -> p (c t)").bitcast(F32).rearrange("p (b r u) -> p b r u", b=2, u=2),
+                in_=bank[:].rearrange("p (b u r) -> p b r u", b=2, u=2),
             )
 
-        def rows_view(src, g):
-            return src[512 * g : 512 * g + 512, :].rearrange("(p t) n -> p t n", t=4)
+        def quantize(codes, planes, values):
+            nc.vector.quantize_mx(
+                out=codes.bitcast(FP8X4), scales=planes, in_=values.rearrange("p c t -> p (c t)")
+            )
 
-        def load_left(g, lo, hi):
-            work_tile(("left", g), [P, 4, K], BF16, "left_rows", 3)
-            nc.sync.dma_start(out=tiles["left", g][:, lo:hi, :], in_=rows_view(left, g)[:, lo:hi, :])
+
+        def load_left(g, t0, t1):
+            rows = rotating("left_rows", g, [P, 4, K], BF16)
+            nc.sync.dma_start(out=rows[:, t0:t1, :], in_=band_rows(left, g)[:, t0:t1, :])
 
         def load_right(h):
-            rows = work_tile(("right", h), [P, 4, 512], BF16, "right_rows", 2)
-            nc.sync.dma_start(
-                out=rows[:], in_=right.rearrange("(p t) n -> p t n", t=4)[:, :, 512 * h : 512 * h + 512]
-            )
+            rows = rotating("right_rows", h, [P, 4, PASS], BF16)
+            nc.sync.dma_start(out=rows[:], in_=band_rows(right, 0)[:, :, half(h)])
 
         def load_d(g, h):
-            rows = work_tile(("d", g), [P, HALVES, 4, 512], BF16, "field_rows", 4)
-            nc.sync.dma_start(out=rows[:, h], in_=rows_view(d, g)[:, :, 512 * h : 512 * h + 512])
+            rows = rotating("field_rows", ("d", g), [P, HALVES, 4, PASS], BF16)
+            nc.sync.dma_start(out=rows[:, h], in_=band_rows(d, g)[:, :, half(h)])
 
         def load_c(g):
-            rows = work_tile(("c", g), [P, 4, N], BF16, "field_rows", 4)
-            nc.sync.dma_start(out=rows[:], in_=rows_view(c, g))
+            rows = rotating("field_rows", ("c", g), [P, 4, N], BF16)
+            nc.sync.dma_start(out=rows[:], in_=band_rows(c, g))
 
         def load_a(pair):
             g, t = pair // 2, 2 * (pair % 2)
-            nc.sync.dma_start(out=code_bytes[g][:, t : t + 2, :], in_=rows_view(a_bytes, g)[:, t : t + 2, :])
+            nc.sync.dma_start(out=code_bytes[g][:, t : t + 2, :], in_=band_rows(a_bytes, g)[:, t : t + 2, :])
 
         def load_a_scale():
             nc.sync.dma_start(
-                out=a_col_scale[:], in_=a_scale.rearrange("o k -> (o k)").partition_broadcast(P)
+                out=column_scale[:], in_=a_scale.rearrange("o k -> (o k)").partition_broadcast(P)
             )
 
+        def clear_b_planes():
+            nc.vector.memset(b_planes[:].rearrange("p h n -> p (h n)").bitcast(I32), 0)
+
         def load_b():
-            nc.sync.dma_start(out=words_b[:], in_=b_words.rearrange("h p n -> p h n"))
+            nc.sync.dma_start(out=b_codes[:], in_=b_words.rearrange("h p n -> p h n"))
             for q in range(4):
                 nc.sync.dma_start(
-                    out=scales_b[32 * q : 32 * q + 4, :, :].bitcast(I32),
+                    out=b_planes[32 * q : 32 * q + 4, :, :].bitcast(I32),
                     in_=b_scales[:, 4 * q : 4 * q + 4, :].rearrange("h r n -> r h n").bitcast(I32),
                 )
 
-        def clear_b_scales():
-            nc.vector.memset(scales_b[:].rearrange("p h n -> p (h n)").bitcast(I32), 0)
-
         def store(i, n0, n1):
-            nc.sync.dma_start(out=rows_view(out, i // 4)[:, i % 4, n0:n1], in_=tiles["result", i][:, n0:n1])
+            nc.sync.dma_start(
+                out=band_rows(out, i // 4)[:, i % 4, n0:n1], in_=held["result", i][:, n0:n1]
+            )
 
-        def left_turn(g, tp):
-            ps = take_bank(("left", g, tp))
-            for tt in range(2):
-                words = tiles["left", g][:, 2 * tp + tt, :].bitcast(F32)
+
+        def left_turn(g, b2):
+            bank = take_bank(("left", g, b2))
+            for b in range(2):
+                words = held["left_rows", g][:, 2 * b2 + b, :].bitcast(F32)
                 for u in range(2):
-                    turn(ps, (2 * tt + u) * P, words[:, u : K // 2 : 2])
+                    transpose(bank, 2 * b + u, words[:, u : K // 2 : 2])
 
-        def left_out(g, tp):
-            copy_words(work_tile(("left_t", g, tp), [P, 256, 4], BF16, "left_t", 2)[:], banks["left", g, tp])
-            drop_bank(("left", g, tp))
+        def left_out(g, b2):
+            key = ("left", g, b2)
+            copy_turned(rotating("left_t", (g, b2), [P, 2 * P, 4], BF16)[:], held["bank", key])
+            give_back(key)
 
-        def left_quantize(g, tp):
-            at = 512 * g + 256 * tp
-            quantize(left_codes[:, at : at + 256], left_scales[:, at : at + 256], tiles["left_t", g, tp])
+        def left_quantize(g, b2):
+            cols = slice(PASS * g + 2 * P * b2, PASS * g + 2 * P * (b2 + 1))
+            quantize(left_codes[:, cols], left_scales[:, cols], held["left_t", (g, b2)][:])
+
 
         def right_interleave(h, u):
-            rt = work_tile(("right_t", h, u), [P, 256, 4], BF16, "right_t", 4)
             copy = nc.scalar.copy if (h, u) == (1, 0) else nc.vector.tensor_copy
             copy(
-                out=rt[:].rearrange("p (q e) t -> p q e t", e=2),
-                in_=tiles["right", h][:].rearrange("p t (q u e) -> p u q e t", u=2, e=2)[:, u],
+                out=rotating("right_t", (h, u), [P, PASS // 2, 4], BF16)[:].rearrange("p (q e) t -> p q e t", e=2),
+                in_=held["right_rows", h][:].rearrange("p t (q u e) -> p u q e t", u=2, e=2)[:, u],
             )
 
         def right_quantize(h, u):
-            cols = slice(512 * h + 256 * u, 512 * h + 256 * u + 256)
-            quantize(right_codes[:, cols], right_scales[:, cols], tiles["right_t", h, u])
+            cols = slice(PASS * h + PASS // 2 * u, PASS * h + PASS // 2 * (u + 1))
+            quantize(right_codes[:, cols], right_scales[:, cols], held["right_t", (h, u)][:])
 
-        x_reads = {}
 
-        def x_read(j, s):
-            x_reads[j, s] = x_reads.get((j, s), 0) + 1
-            if x_reads[j, s] == 2:
-                drop_bank(("x", j, s))
+        slice_reads = {}
+
+        def slice_read(j, s):
+            slice_reads[j, s] = slice_reads.get((j, s), 0) + 1
+            if slice_reads[j, s] == 2:
+                give_back(("x", j, s))
 
         def x_matmul(j, s):
             g, h = j // 2, j % 2
-            ps = take_bank(("x", j, s))
-            cols = slice(512 * h + P * s, 512 * h + P * s + P)
+            bank = take_bank(("x", j, s))
+            cols = slice(PASS * h + P * s, PASS * h + P * (s + 1))
             for t in range(4):
-                rows = slice(512 * g + P * t, 512 * g + P * t + P)
+                rows = slice(PASS * g + P * t, PASS * g + P * (t + 1))
                 nc.tensor.matmul_mx(
-                    out=ps[:, P * t : P * t + P],
+                    out=bank[:, P * t : P * (t + 1)],
                     lhsT=left_codes[:, rows].bitcast(FP8X4),
                     lhsT_scale=left_scales[:, rows],
                     rhs=right_codes[:, cols].bitcast(FP8X4),
@@ -180,223 +204,286 @@ def tile_sylvester_scaled_residual_s8_kernel(
                 )
 
         def x_out(j, s):
-            work_tile(("x_t", j), [P, 512, 4], BF16, "x_t", 4)
-            u, half = s // 2, s % 2
+            u, v = s // 2, s % 2
+            x_t = rotating("x_t", j, [P, PASS, 4], BF16)
             nc.scalar.copy(
-                out=tiles["x_t", j][:].rearrange("p (q u e) t -> p u q e t", u=2, e=2)[:, u, 64 * half : 64 * half + 64],
-                in_=banks["x", j, s][:].rearrange("p (t q e) -> p q e t", t=4, e=2),
+                out=x_t[:].rearrange("p (q u e) t -> p u q e t", u=2, e=2)[:, u, 64 * v : 64 * (v + 1)],
+                in_=held["bank", ("x", j, s)][:].rearrange("p (t q e) -> p q e t", t=4, e=2),
             )
-            x_read(j, s)
+            slice_read(j, s)
 
         def x_quantize(j):
-            g, cols = j // 2, slice(512 * (j % 2), 512 * (j % 2) + 512)
-            quantize(x_codes[:, g, cols], x_scales[:, g, cols], tiles["x_t", j])
+            g, h = j // 2, j % 2
+            quantize(x_codes[:, g, half(h)], x_scales[:, g, half(h)], held["x_t", j][:])
 
         def y_multiply(j, s):
-            work_tile(("y_rows", j), [P, 4, 2, 256], BF16, "y_rows", 3)
             g, h = j // 2, j % 2
-            u, half = s // 2, s % 2
+            u, v = s // 2, s % 2
+            y_rows = rotating("y_rows", j, [P, 4, 2, PASS // 2], BF16)
             nc.vector.tensor_tensor(
-                out=tiles["y_rows", j][:, :, u, P * half : P * half + P].rearrange("p t (q e) -> p t q e", e=2),
-                in0=banks["x", j, s][:].rearrange("p (t q e) -> p t q e", t=4, e=2),
-                in1=tiles["d", g][:, h].rearrange("p t (q u e) -> p u t q e", u=2, e=2)[
-                    :, u, :, 64 * half : 64 * half + 64
+                out=y_rows[:, :, u, P * v : P * (v + 1)].rearrange("p t (q e) -> p t q e", e=2),
+                in0=held["bank", ("x", j, s)][:].rearrange("p (t q e) -> p t q e", t=4, e=2),
+                in1=held["field_rows", ("d", g)][:, h].rearrange("p t (q u e) -> p u t q e", u=2, e=2)[
+                    :, u, :, 64 * v : 64 * (v + 1)
                 ],
                 op=MULT,
             )
-            x_read(j, s)
+            slice_read(j, s)
 
-        def y_turn(j, tp):
-            ps = take_bank(("y", j, tp))
-            for tt in range(2):
+        def y_turn(j, b2):
+            bank = take_bank(("y", j, b2))
+            for b in range(2):
                 for u in range(2):
-                    turn(ps, (2 * tt + u) * P, tiles["y_rows", j][:, 2 * tp + tt, u, :].bitcast(F32))
+                    transpose(bank, 2 * b + u, held["y_rows", j][:, 2 * b2 + b, u, :].bitcast(F32))
 
-        def y_out(j, tp):
-            work_tile(("y_t", j), [P, 512, 4], BF16, "y_t", 2)
-            copy_words(tiles["y_t", j][:, 256 * tp : 256 * tp + 256, :], banks["y", j, tp])
-            drop_bank(("y", j, tp))
+        def y_out(j, b2):
+            y_t = rotating("y_t", j, [P, PASS, 4], BF16)
+            copy_turned(y_t[:, 2 * P * b2 : 2 * P * (b2 + 1), :], held["bank", ("y", j, b2)])
+            give_back(("y", j, b2))
 
         def y_quantize(j):
-            h, cols = j % 2, slice(512 * (j // 2), 512 * (j // 2) + 512)
-            quantize(y_codes[:, h, cols], y_scales[:, h, cols], tiles["y_t", j])
+            g, h = j // 2, j % 2
+            quantize(y_codes[:, h, half(g)], y_scales[:, h, half(g)], held["y_t", j][:])
+
 
         def a_multiply(i):
-            vals = work_tile(("a_values", i), [P, M], BF16, "a_values", 2)
             nc.vector.tensor_tensor(
-                out=vals[:], in0=code_bytes[i // 4][:, i % 4, :].bitcast(FP8), in1=a_col_scale[:], op=MULT
+                out=rotating("a_values", i, [P, M], BF16)[:],
+                in0=code_bytes[i // 4][:, i % 4, :].bitcast(FP8),
+                in1=column_scale[:],
+                op=MULT,
             )
 
         def a_reorder(i):
             nc.scalar.copy(
-                out=work_tile(("a_words", i), [P, GROUPS, 2, P], F32, "a_words", 4)[:],
-                in_=tiles["a_values", i][:].bitcast(F32).rearrange("p (g q u) -> p g u q", g=GROUPS, u=2),
+                out=rotating("a_words", i, [P, GROUPS, 2, P], F32)[:],
+                in_=held["a_values", i][:].bitcast(F32).rearrange("p (g q u) -> p g u q", g=GROUPS, u=2),
             )
 
         def a_turn(pair, g):
-            ps = take_bank(("a", pair, g))
-            for tt in range(2):
+            bank = take_bank(("a", pair, g))
+            for b in range(2):
                 for u in range(2):
-                    turn(ps, (2 * tt + u) * P, tiles["a_words", 2 * pair + tt][:, g, u, :])
+                    transpose(bank, 2 * b + u, held["a_words", 2 * pair + b][:, g, u, :])
 
         def a_out(pair, g):
-            copy_words(work_tile(("a_t", pair, g), [P, 256, 4], BF16, "a_t", 4)[:], banks["a", pair, g])
-            drop_bank(("a", pair, g))
+            key = ("a", pair, g)
+            copy_turned(rotating("a_t", (pair, g), [P, 2 * P, 4], BF16)[:], held["bank", key])
+            give_back(key)
 
         def a_quantize(pair, g):
-            cols = slice(256 * pair, 256 * pair + 256)
-            quantize(a_codes[:, g, cols], a_scales[:, g, cols], tiles["a_t", pair, g])
+            cols = slice(2 * P * pair, 2 * P * (pair + 1))
+            quantize(a_codes[:, g, cols], a_scales[:, g, cols], held["a_t", (pair, g)][:])
 
-        def y_pass(i, n0, h, out, width, **flags):
-            rows = slice(P * i, P * i + P)
+
+        def multiply_y(i, n0, h, width, **group):
+            rows = slice(P * i, P * (i + 1))
             nc.tensor.matmul_mx(
-                out=out,
                 lhsT=y_codes[:, h, rows].bitcast(FP8X4),
                 lhsT_scale=y_scales[:, h, rows],
-                rhs=words_b[:, h, 2 * n0 : 2 * n0 + 2 * width].bitcast(FP4X4),
-                rhs_scale=scales_b[:, h, n0 : n0 + width],
-                **flags,
+                rhs=b_codes[:, h, 2 * n0 : 2 * (n0 + width)].bitcast(FP4X4),
+                rhs_scale=b_planes[:, h, n0 : n0 + width],
+                **group,
             )
 
-        def a_pass(i, n0, g, out, width, **flags):
-            rows = slice(P * i, P * i + P)
+        def multiply_a(i, n0, g, width, **group):
+            rows = slice(P * i, P * (i + 1))
             nc.tensor.matmul_mx(
-                out=out,
                 lhsT=a_codes[:, g, rows].bitcast(FP8X4),
                 lhsT_scale=a_scales[:, g, rows],
                 rhs=x_codes[:, g, n0 : n0 + width].bitcast(FP8X4),
                 rhs_scale=x_scales[:, g, n0 : n0 + width],
-                **flags,
+                **group,
             )
 
-        passes = {}
+        passes_done = {}
 
-        def wide_flags(i, n0):
-            passes[i, n0] = passes.get((i, n0), 0) + 1
-            if passes[i, n0] == 1:
+        def next_pass(i, n0):
+            count = passes_done.get((i, n0), 0) + 1
+            passes_done[i, n0] = count
+            if count == 1:
                 take_bank(("out", i, n0))
             return dict(
-                out=banks["out", i, n0][:],
-                width=512,
-                start=(passes[i, n0] == 1),
-                stop=(passes[i, n0] == HALVES + GROUPS),
+                width=PASS,
+                out=held["bank", ("out", i, n0)][:],
+                start=(count == 1),
+                stop=(count == HALVES + GROUPS),
             )
 
-        def wide_y(i, n0, h):
-            y_pass(i, n0, h, **wide_flags(i, n0))
+        def y_pass(i, n0, h):
+            multiply_y(i, n0, h, **next_pass(i, n0))
 
-        def wide_a(i, n0, g):
-            a_pass(i, n0, g, **wide_flags(i, n0))
+        def a_pass(i, n0, g):
+            multiply_a(i, n0, g, **next_pass(i, n0))
 
-        def narrow(i, n0):
-            if n0 % 256 == 0:
-                take_bank(("out", i, n0))
-            at = n0 % 256
-            ps = banks["out", i, n0 - at][:, at : at + P]
+        def narrow_sum(i, n0):
+            bank0 = n0 - n0 % (2 * P)
+            if n0 == bank0:
+                take_bank(("out", i, bank0))
+            piece = held["bank", ("out", i, bank0)][:, n0 - bank0 : n0 - bank0 + P]
             for h in range(HALVES):
-                y_pass(i, n0, h, ps, P, start=(h == 0), stop=False)
+                multiply_y(i, n0, h, width=P, out=piece, start=(h == 0), stop=False)
             for g in range(GROUPS):
-                a_pass(i, n0, g, ps, P, start=False, stop=(g == GROUPS - 1))
+                multiply_a(i, n0, g, width=P, out=piece, start=False, stop=(g == GROUPS - 1))
 
         def subtract_c(i, n0, n1):
-            work_tile(("result", i), [P, N], F32, "result", 4)
             nc.vector.tensor_tensor(
-                out=tiles["result", i][:, n0:n1],
-                in0=banks["out", i, n0][:, : n1 - n0],
-                in1=tiles["c", i // 4][:, i % 4, n0:n1],
-                op=SUB,
+                out=rotating("result", i, [P, N], F32)[:, n0:n1],
+                in0=held["bank", ("out", i, n0)][:, : n1 - n0],
+                in1=held["field_rows", ("c", i // 4)][:, i % 4, n0:n1],
+                op=SUBTRACT,
             )
-            drop_bank(("out", i, n0))
+            give_back(("out", i, n0))
 
-        def needs(step):
-            f, x = step[0], step[1:]
-            if f == left_turn:
-                return [(load_left, 0, 2 * x[1], 2 * x[1] + 2)] if x[0] == 0 else [(load_left, x[0], 0, 4)]
-            if f == left_out:
-                n = 2 * x[0] + x[1] - 2
-                return [(left_turn,) + x] + ([(left_quantize, n // 2, n % 2)] if n >= 0 else [])
-            if f == left_quantize:
-                return [(left_out,) + x]
-            if f == right_interleave:
-                return [(load_right, x[0])]
-            if f == right_quantize:
-                return [(right_interleave,) + x]
-            if f == x_matmul:
-                return [(left_quantize, x[0] // 2, tp) for tp in range(2)] + [(right_quantize, x[0] % 2, x[1] // 2)]
-            if f == x_out:
-                return [(x_matmul,) + x] + ([(x_quantize, x[0] - 4)] if x[0] > 3 else [])
-            if f == y_multiply:
-                return [(x_matmul,) + x, (load_d, x[0] // 2, x[0] % 2)] + ([(y_turn, x[0] - 3, 1)] if x[0] > 2 else [])
-            if f == x_quantize:
-                return [(x_out, x[0], s) for s in range(4)]
-            if f == y_turn:
-                return [(y_multiply, x[0], s) for s in range(4)]
-            if f == y_out:
-                return [(y_turn,) + x] + ([(y_quantize, x[0] - 2)] if x[0] > 1 else [])
-            if f == y_quantize:
-                return [(y_out, x[0], tp) for tp in range(2)]
-            if f == a_multiply:
-                return [(load_a_scale,), (load_a, x[0] // 2)] + ([(a_reorder, x[0] - 2)] if x[0] > 1 else [])
-            if f == a_reorder:
-                return [(a_multiply,) + x] + ([(a_turn, x[0] // 2 - 2, GROUPS - 1)] if x[0] > 3 else [])
-            if f == a_turn:
-                return [(a_reorder, 2 * x[0] + tt) for tt in range(2)]
-            if f == a_out:
-                n = 3 * x[0] + x[1] - 4
-                return [(a_turn,) + x] + ([(a_quantize, n // 3, n % 3)] if n >= 0 else [])
-            if f == a_quantize:
-                return [(a_out,) + x]
-            if f == wide_y:
-                return [(y_quantize, 2 * (x[0] // 4) + x[2]), (load_b,)]
-            if f == wide_a:
-                return [(a_quantize, x[0] // 2, x[2]), (x_quantize, 2 * x[2] + x[1] // 512)]
-            if f == narrow:
-                return [(a_quantize, x[0] // 2, GROUPS - 1), (y_quantize, 2 * GROUPS - 1)]
-            if f == subtract_c:
-                i, n0, n1 = x
-                made = [(narrow, i, n0), (narrow, i, n0 + P)]
-                if n1 - n0 == 512:
-                    made = [(wide_y, i, n0, h) for h in range(HALVES)] + [(wide_a, i, n0, g) for g in range(GROUPS)]
-                return made + [(load_c, i // 4)] + ([(store, i - 4, 0, N)] if i > 3 else [])
-            if f == store:
-                i, n0, n1 = x
-                return [(subtract_c, i, 0, 512), (subtract_c, i, 512, N)] if n1 - n0 == N else [(subtract_c,) + x]
-            if f == load_b:
-                return [(clear_b_scales,)]
-            if f == load_c and x[0] > 0:
-                return [(y_multiply, 2 * x[0] - 2 + h, s) for h in range(HALVES) for s in range(4)]
-            return []
 
-        TAKES_BANK = (left_turn, x_matmul, y_turn, a_turn)
+        def both(f, *x):
+            return [(f, *x, 0), (f, *x, 1)]
+
+        def freed(name, n, last_reads):
+            return last_reads(n - DEPTH[name]) if n >= DEPTH[name] else []
+
+        def slices(f, j):
+            return [(f, j, s) for s in range(4)]
+
+        def sums(i, n0, n1):
+            if n1 - n0 < PASS:
+                return [(narrow_sum, i, n0), (narrow_sum, i, n0 + P)]
+            return [(y_pass, i, n0, h) for h in range(HALVES)] + [(a_pass, i, n0, g) for g in range(GROUPS)]
+
+        after = {
+            left_turn: lambda g, b2: [(load_left, g, 2 * b2, 2 * b2 + 2) if g == 0 else (load_left, g, 0, 4)],
+            left_out: lambda g, b2: [(left_turn, g, b2)]
+            + freed("left_t", 2 * g + b2, lambda n: [(left_quantize, n // 2, n % 2)]),
+            left_quantize: lambda g, b2: [(left_out, g, b2)],
+            right_interleave: lambda h, u: [(load_right, h)],
+            right_quantize: lambda h, u: [(right_interleave, h, u)],
+            x_matmul: lambda j, s: both(left_quantize, j // 2) + [(right_quantize, j % 2, s // 2)],
+            x_out: lambda j, s: [(x_matmul, j, s)] + freed("x_t", j, lambda n: [(x_quantize, n)]),
+            x_quantize: lambda j: slices(x_out, j),
+            y_multiply: lambda j, s: [(x_matmul, j, s), (load_d, j // 2, j % 2)]
+            + freed("y_rows", j, lambda n: both(y_turn, n)),
+            y_turn: lambda j, b2: slices(y_multiply, j),
+            y_out: lambda j, b2: [(y_turn, j, b2)] + freed("y_t", j, lambda n: [(y_quantize, n)]),
+            y_quantize: lambda j: both(y_out, j),
+            a_multiply: lambda i: [(load_a_scale,), (load_a, i // 2)]
+            + freed("a_values", i, lambda n: [(a_reorder, n)]),
+            a_reorder: lambda i: [(a_multiply, i)]
+            + freed("a_words", i, lambda n: [(a_turn, n // 2, g) for g in range(GROUPS)]),
+            a_turn: lambda pair, g: both_bands(a_reorder, pair),
+            a_out: lambda pair, g: [(a_turn, pair, g)]
+            + freed("a_t", GROUPS * pair + g, lambda n: [(a_quantize, n // GROUPS, n % GROUPS)]),
+            a_quantize: lambda pair, g: [(a_out, pair, g)],
+            y_pass: lambda i, n0, h: [(load_b,), (y_quantize, 2 * (i // 4) + h)],
+            a_pass: lambda i, n0, g: [(a_quantize, i // 2, g), (x_quantize, 2 * g + n0 // PASS)],
+            narrow_sum: lambda i, n0: [(load_b,)]
+            + [(y_quantize, 2 * (i // 4) + h) for h in range(HALVES)]
+            + [(a_quantize, i // 2, g) for g in range(GROUPS)]
+            + [(x_quantize, 2 * g + n0 // PASS) for g in range(GROUPS)],
+            subtract_c: lambda i, n0, n1: sums(i, n0, n1)
+            + [(load_c, i // 4)]
+            + freed("result", i, lambda n: [(store, n, 0, N)]),
+            store: lambda i, n0, n1: both_halves(i) if n1 - n0 == N else [(subtract_c, i, n0, n1)],
+            load_b: lambda: [(clear_b_planes,)],
+            load_c: lambda g: freed("field_rows", GROUPS + g, lambda n: slices(y_multiply, 2 * n) + slices(y_multiply, 2 * n + 1)),
+        }
+
+        def both_bands(f, pair):
+            return [(f, 2 * pair), (f, 2 * pair + 1)]
+
+        def both_halves(i):
+            return [(subtract_c, i, PASS * n, PASS * (n + 1)) for n in range(HALVES)]
+
+        def opens_bank(f, x):
+            if f in (y_pass, a_pass):
+                return x[:2] not in passes_done
+            if f == narrow_sum:
+                return x[1] % (2 * P) == 0
+            return f in (left_turn, x_matmul, y_turn, a_turn)
 
         def issue(queues):
-            left_over = [list(q) for q in queues]
+            waiting = [list(q) for q in queues]
             issued = set()
-            while any(left_over):
-                stuck = True
-                for q in left_over:
+            while any(waiting):
+                before = len(issued)
+                for q in waiting:
                     if not q:
                         continue
-                    step = q[0]
-                    f, x = step[0], step[1:]
-                    opens = (
-                        f in TAKES_BANK
-                        or (f in (wide_y, wide_a) and x[:2] not in passes)
-                        or (f == narrow and x[1] % 256 == 0)
-                    )
-                    if (opens and not free_banks) or any(s not in issued for s in needs(step)):
-                        continue
-                    f(*x)
-                    issued.add(step)
-                    q.pop(0)
-                    stuck = False
-                assert not stuck, [q[0] for q in left_over if q]
+                    f, x = q[0][0], q[0][1:]
+                    ready = all(s in issued for s in (after[f](*x) if f in after else []))
+                    if ready and (free_banks or not opens_bank(f, x)):
+                        f(*x)
+                        issued.add(q.pop(0))
+                assert len(issued) > before
+
+
+        def units(f, pair):
+            return [(f, pair, g) for g in range(GROUPS)]
+
+        def y_passes(i):
+            return [(y_pass, i, PASS * n, h) for h in range(HALVES) for n in range(HALVES)]
+
+        def a_passes(i, *groups):
+            return [(a_pass, i, PASS * n, g) for g in groups for n in range(HALVES)]
+
+        def some(f, j, *picked):
+            return [(f, j, s) for s in picked]
+
+        pairs = BANDS // 2
+        loads = [(load_left, 0, 0, 2), (load_left, 0, 2, 4), (load_right, 0), (load_right, 1)]
+        loads += [(load_left, 1, 0, 4), (load_d, 0, 0), (load_a, 0), (load_d, 0, 1), (load_left, 2, 0, 4)]
+        loads += [(load_a_scale,)] + both(load_d, 1) + [(load_a, 1), (load_b,), (load_a, 2)] + both(load_d, 2)
+        loads += [(load_c, 0), (load_c, 1), (load_a, 3), (load_a, 4), (load_c, 2), (load_a, 5)]
+        loads += [(store, i, 0, N) for i in range(LAST)]
+        loads += [(store, LAST, 0, PASS), (store, LAST, PASS, PASS + 2 * P), (store, LAST, PASS + 2 * P, N)]
+
+        tensor = both(left_turn, 0) + some(x_matmul, 0, 0, 1) + both(left_turn, 1)
+        tensor += slices(x_matmul, 1) + some(x_matmul, 0, 2, 3) + both(left_turn, 2) + both(y_turn, 0)
+        tensor += slices(x_matmul, 2) + slices(x_matmul, 3) + both(y_turn, 1)
+        tensor += some(x_matmul, 4, 0, 1) + units(a_turn, 0) + some(x_matmul, 4, 2, 3) + both(y_turn, 2)
+        tensor += some(x_matmul, 5, 0, 1) + y_passes(0) + some(x_matmul, 5, 2, 3)
+        tensor += a_passes(0, 0, 1) + y_passes(1) + a_passes(1, 0) + units(a_turn, 1) + a_passes(1, 1)
+        tensor += both(y_turn, 3) + both(y_turn, 4) + a_passes(0, 2) + y_passes(2) + a_passes(1, 2)
+        tensor += a_passes(2, 0, 1, 2) + both(y_turn, 5) + units(a_turn, 2) + y_passes(3) + a_passes(3, 0, 1, 2)
+        for pair in range(2, pairs - 1):
+            tensor += y_passes(2 * pair) + a_passes(2 * pair, 0, 1, 2)
+            tensor += y_passes(2 * pair + 1) + a_passes(2 * pair + 1, 0)
+            tensor += units(a_turn, pair + 1) + a_passes(2 * pair + 1, 1, 2)
+        tensor += y_passes(LAST - 1) + a_passes(LAST - 1, 0, 1, 2)
+        tensor += sums(LAST, 0, PASS) + [(narrow_sum, LAST, n0) for n0 in range(PASS, N, P)]
+
+        scalar = both(left_out, 0) + [(right_interleave, 1, 0)] + some(x_out, 0, 0, 1) + both(left_out, 1)
+        scalar += some(x_out, 0, 2, 3) + some(x_out, 1, 0) + both(left_out, 2) + some(x_out, 1, 1, 2, 3)
+        scalar += both(y_out, 0) + slices(x_out, 2) + [(a_reorder, 0)] + some(x_out, 3, 0, 1, 2)
+        scalar += both(y_out, 1) + [(a_reorder, 1)] + some(x_out, 3, 3) + some(x_out, 4, 0, 1)
+        scalar += units(a_out, 0) + some(x_out, 4, 2, 3) + [(a_reorder, 2)] + both(y_out, 2)
+        scalar += slices(x_out, 5) + [(a_reorder, 3)] + units(a_out, 1) + both(y_out, 3) + both(y_out, 4)
+        scalar += both_bands(a_reorder, 2) + units(a_out, 2) + both(y_out, 5)
+        for pair in range(3, pairs):
+            scalar += both_bands(a_reorder, pair) + units(a_out, pair)
+
+        vector = [(clear_b_planes,), (right_interleave, 0, 0)] + both(left_quantize, 0) + [(right_quantize, 0, 0)]
+        vector += [(right_interleave, 0, 1), (right_interleave, 1, 1)]
+        vector += [(right_quantize, 0, 1), (right_quantize, 1, 1), (right_quantize, 1, 0)]
+        vector += some(y_multiply, 0, 0, 1) + some(y_multiply, 1, 0) + both(left_quantize, 1)
+        vector += some(y_multiply, 1, 1, 2, 3) + some(y_multiply, 0, 2, 3) + both(left_quantize, 2)
+        vector += [(x_quantize, 0), (a_multiply, 0)] + some(y_multiply, 2, 0) + [(x_quantize, 1)]
+        vector += some(y_multiply, 2, 1, 2) + [(y_quantize, 0), (a_multiply, 1)] + some(y_multiply, 2, 3)
+        vector += some(y_multiply, 3, 0, 1, 3, 2) + [(a_multiply, 2), (x_quantize, 2)]
+        vector += some(y_multiply, 4, 0, 1) + [(x_quantize, 3), (y_quantize, 1)] + units(a_quantize, 0)
+        vector += some(y_multiply, 4, 2, 3) + [(a_multiply, 3)] + slices(y_multiply, 5)
+        vector += [(x_quantize, 4), (x_quantize, 5)] + units(a_quantize, 1) + [(y_quantize, 2)]
+        vector += both_bands(a_multiply, 2) + both_halves(0) + both_halves(1) + [(y_quantize, 3), (a_multiply, 6)]
+        vector += units(a_quantize, 2) + both_halves(2) + [(y_quantize, 4), (a_multiply, 7), (y_quantize, 5)]
+        vector += both_halves(3)
+        for pair in range(4, pairs):
+            vector += [(a_multiply, 2 * pair)] + units(a_quantize, pair - 1) + [(a_multiply, 2 * pair + 1)]
+            vector += both_halves(2 * pair - 4) + both_halves(2 * pair - 3)
+        vector += units(a_quantize, pairs - 1)
+        for i in range(2 * pairs - 4, LAST):
+            vector += both_halves(i)
+        vector += [(subtract_c, LAST, 0, PASS)]
+        vector += [(subtract_c, LAST, n0, n0 + 2 * P) for n0 in range(PASS, N, 2 * P)]
 
         make_identity(nc, ident[:])
         with tc.manual_schedule():
-            issue((
-                [(load_left, 0, 0, 2), (load_left, 0, 2, 4), (load_right, 0), (load_right, 1), (load_left, 1, 0, 4), (load_d, 0, 0), (load_d, 0, 1), (load_left, 2, 0, 4), (load_a_scale,), (load_a, 0), (load_d, 1, 0), (load_d, 1, 1), (load_a, 1), (load_b,), (load_a, 2), (load_d, 2, 0), (load_d, 2, 1), (load_c, 0), (load_c, 1), (load_a, 3), (load_a, 4), (load_c, 2), (load_a, 5), (store, 0, 0, N), (store, 1, 0, N), (store, 2, 0, N), (store, 3, 0, N), (store, 4, 0, N), (store, 5, 0, N), (store, 6, 0, N), (store, 7, 0, N), (store, 8, 0, N), (store, 9, 0, N), (store, 10, 0, N), (store, 11, 0, 512), (store, 11, 512, 768), (store, 11, 768, 1024)],
-                [(left_turn, 0, 0,), (left_turn, 0, 1,), (x_matmul, 0, 0,), (x_matmul, 0, 1,), (left_turn, 1, 0,), (left_turn, 1, 1,), (x_matmul, 1, 0,), (x_matmul, 1, 1,), (x_matmul, 1, 2,), (x_matmul, 1, 3,), (x_matmul, 0, 2,), (x_matmul, 0, 3,), (left_turn, 2, 0,), (left_turn, 2, 1,), (y_turn, 0, 0,), (y_turn, 0, 1,), (x_matmul, 2, 0,), (x_matmul, 2, 1,), (x_matmul, 2, 2,), (x_matmul, 2, 3,), (x_matmul, 3, 0,), (x_matmul, 3, 1,), (x_matmul, 3, 2,), (x_matmul, 3, 3,), (y_turn, 1, 0,), (y_turn, 1, 1,), (x_matmul, 4, 0,), (x_matmul, 4, 1,), (a_turn, 0, 0,), (a_turn, 0, 1,), (a_turn, 0, 2,), (x_matmul, 4, 2,), (x_matmul, 4, 3,), (y_turn, 2, 0,), (y_turn, 2, 1,), (x_matmul, 5, 0,), (x_matmul, 5, 1,), (wide_y, 0, 0, 0), (wide_y, 0, 512, 0), (wide_y, 0, 0, 1), (wide_y, 0, 512, 1), (x_matmul, 5, 2,), (x_matmul, 5, 3,), (wide_a, 0, 0, 0), (wide_a, 0, 512, 0), (wide_a, 0, 0, 1), (wide_a, 0, 512, 1), (wide_y, 1, 0, 0), (wide_y, 1, 512, 0), (wide_y, 1, 0, 1), (wide_y, 1, 512, 1), (wide_a, 1, 0, 0), (wide_a, 1, 512, 0), (a_turn, 1, 0,), (a_turn, 1, 1,), (a_turn, 1, 2,), (wide_a, 1, 0, 1), (wide_a, 1, 512, 1), (y_turn, 3, 0,), (y_turn, 3, 1,), (y_turn, 4, 0,), (y_turn, 4, 1,), (wide_a, 0, 0, 2), (wide_a, 0, 512, 2), (wide_y, 2, 0, 0), (wide_y, 2, 512, 0), (wide_y, 2, 0, 1), (wide_y, 2, 512, 1), (wide_a, 1, 0, 2), (wide_a, 1, 512, 2), (wide_a, 2, 0, 0), (wide_a, 2, 512, 0), (wide_a, 2, 0, 1), (wide_a, 2, 512, 1), (wide_a, 2, 0, 2), (wide_a, 2, 512, 2), (y_turn, 5, 0,), (y_turn, 5, 1,), (a_turn, 2, 0,), (a_turn, 2, 1,), (a_turn, 2, 2,), (wide_y, 3, 0, 0), (wide_y, 3, 512, 0), (wide_y, 3, 0, 1), (wide_y, 3, 512, 1), (wide_a, 3, 0, 0), (wide_a, 3, 512, 0), (wide_a, 3, 0, 1), (wide_a, 3, 512, 1), (wide_a, 3, 0, 2), (wide_a, 3, 512, 2), (wide_y, 4, 0, 0), (wide_y, 4, 512, 0), (wide_y, 4, 0, 1), (wide_y, 4, 512, 1), (wide_a, 4, 0, 0), (wide_a, 4, 512, 0), (wide_a, 4, 0, 1), (wide_a, 4, 512, 1), (wide_a, 4, 0, 2), (wide_a, 4, 512, 2), (wide_y, 5, 0, 0), (wide_y, 5, 512, 0), (wide_y, 5, 0, 1), (wide_y, 5, 512, 1), (wide_a, 5, 0, 0), (wide_a, 5, 512, 0), (a_turn, 3, 0,), (a_turn, 3, 1,), (a_turn, 3, 2,), (wide_a, 5, 0, 1), (wide_a, 5, 512, 1), (wide_a, 5, 0, 2), (wide_a, 5, 512, 2), (wide_y, 6, 0, 0), (wide_y, 6, 512, 0), (wide_y, 6, 0, 1), (wide_y, 6, 512, 1), (wide_a, 6, 0, 0), (wide_a, 6, 512, 0), (wide_a, 6, 0, 1), (wide_a, 6, 512, 1), (wide_a, 6, 0, 2), (wide_a, 6, 512, 2), (wide_y, 7, 0, 0), (wide_y, 7, 512, 0), (wide_y, 7, 0, 1), (wide_y, 7, 512, 1), (wide_a, 7, 0, 0), (wide_a, 7, 512, 0), (wide_a, 7, 0, 1), (wide_a, 7, 512, 1), (a_turn, 4, 0,), (a_turn, 4, 1,), (a_turn, 4, 2,), (wide_a, 7, 0, 2), (wide_a, 7, 512, 2), (wide_a, 8, 0, 0), (wide_a, 8, 512, 0), (wide_a, 8, 0, 1), (wide_a, 8, 512, 1), (wide_a, 8, 0, 2), (wide_a, 8, 512, 2), (wide_y, 8, 0, 0), (wide_y, 8, 512, 0), (wide_y, 8, 0, 1), (wide_y, 8, 512, 1), (wide_y, 9, 0, 0), (wide_y, 9, 512, 0), (wide_y, 9, 0, 1), (wide_y, 9, 512, 1), (a_turn, 5, 0,), (a_turn, 5, 1,), (a_turn, 5, 2,), (wide_a, 9, 0, 0), (wide_a, 9, 512, 0), (wide_a, 9, 0, 1), (wide_a, 9, 512, 1), (wide_a, 9, 0, 2), (wide_a, 9, 512, 2), (wide_y, 10, 0, 0), (wide_y, 10, 512, 0), (wide_y, 10, 0, 1), (wide_y, 10, 512, 1), (wide_a, 10, 0, 0), (wide_a, 10, 512, 0), (wide_a, 10, 0, 1), (wide_a, 10, 512, 1), (wide_a, 10, 0, 2), (wide_a, 10, 512, 2), (wide_y, 11, 0, 0), (wide_y, 11, 0, 1), (wide_a, 11, 0, 0), (wide_a, 11, 0, 1), (wide_a, 11, 0, 2), (narrow, 11, 512), (narrow, 11, 640), (narrow, 11, 768), (narrow, 11, 896)],
-                [(left_out, 0, 0,), (left_out, 0, 1,), (right_interleave, 1, 0,), (x_out, 0, 0,), (x_out, 0, 1,), (left_out, 1, 0,), (left_out, 1, 1,), (x_out, 0, 2,), (x_out, 0, 3,), (x_out, 1, 0,), (left_out, 2, 0,), (left_out, 2, 1,), (x_out, 1, 1,), (x_out, 1, 2,), (x_out, 1, 3,), (y_out, 0, 0,), (y_out, 0, 1,), (x_out, 2, 1,), (x_out, 2, 2,), (x_out, 2, 3,), (x_out, 2, 0,), (a_reorder, 0,), (x_out, 3, 0,), (x_out, 3, 1,), (x_out, 3, 2,), (y_out, 1, 0,), (y_out, 1, 1,), (a_reorder, 1,), (x_out, 3, 3,), (x_out, 4, 0,), (x_out, 4, 1,), (a_out, 0, 0,), (a_out, 0, 1,), (a_out, 0, 2,), (x_out, 4, 2,), (x_out, 4, 3,), (a_reorder, 2,), (y_out, 2, 0,), (y_out, 2, 1,), (x_out, 5, 0,), (x_out, 5, 1,), (x_out, 5, 2,), (x_out, 5, 3,), (a_reorder, 3,), (a_out, 1, 0,), (a_out, 1, 1,), (a_out, 1, 2,), (y_out, 3, 0,), (y_out, 3, 1,), (y_out, 4, 0,), (y_out, 4, 1,), (a_reorder, 4,), (a_reorder, 5,), (a_out, 2, 0,), (a_out, 2, 1,), (a_out, 2, 2,), (a_reorder, 6,), (y_out, 5, 0,), (y_out, 5, 1,), (a_reorder, 7,), (a_out, 3, 0,), (a_out, 3, 1,), (a_out, 3, 2,), (a_reorder, 8,), (a_reorder, 9,), (a_out, 4, 0,), (a_out, 4, 1,), (a_out, 4, 2,), (a_reorder, 10,), (a_reorder, 11,), (a_out, 5, 0,), (a_out, 5, 1,), (a_out, 5, 2,)],
-                [(clear_b_scales,), (right_interleave, 0, 0,), (left_quantize, 0, 0,), (left_quantize, 0, 1,), (right_quantize, 0, 0,), (right_interleave, 0, 1,), (right_interleave, 1, 1,), (right_quantize, 0, 1,), (right_quantize, 1, 1,), (right_quantize, 1, 0,), (y_multiply, 0, 0,), (y_multiply, 0, 1,), (y_multiply, 1, 0,), (left_quantize, 1, 0,), (left_quantize, 1, 1,), (y_multiply, 1, 3,), (y_multiply, 0, 2,), (y_multiply, 0, 3,), (y_multiply, 1, 1,), (y_multiply, 1, 2,), (left_quantize, 2, 0,), (left_quantize, 2, 1,), (x_quantize, 0,), (a_multiply, 0,), (y_multiply, 2, 0,), (x_quantize, 1,), (y_multiply, 2, 2,), (y_multiply, 2, 1,), (y_quantize, 0), (a_multiply, 1,), (y_multiply, 2, 3,), (y_multiply, 3, 0,), (y_multiply, 3, 1,), (y_multiply, 3, 3,), (y_multiply, 3, 2,), (a_multiply, 2,), (x_quantize, 2,), (y_multiply, 4, 0,), (y_multiply, 4, 1,), (x_quantize, 3,), (y_quantize, 1), (a_quantize, 0, 0,), (a_quantize, 0, 1,), (y_multiply, 4, 2,), (y_multiply, 4, 3,), (a_quantize, 0, 2,), (a_multiply, 3,), (y_multiply, 5, 0,), (y_multiply, 5, 1,), (y_multiply, 5, 2,), (y_multiply, 5, 3,), (x_quantize, 4,), (x_quantize, 5,), (a_quantize, 1, 0,), (a_quantize, 1, 1,), (a_quantize, 1, 2,), (y_quantize, 2), (a_multiply, 4,), (a_multiply, 5,), (subtract_c, 0, 0, 512), (subtract_c, 0, 512, 1024), (subtract_c, 1, 0, 512), (subtract_c, 1, 512, 1024), (y_quantize, 3), (a_multiply, 6,), (a_quantize, 2, 0,), (subtract_c, 2, 0, 512), (subtract_c, 2, 512, 1024), (a_quantize, 2, 1,), (a_quantize, 2, 2,), (y_quantize, 4), (a_multiply, 7,), (y_quantize, 5), (subtract_c, 3, 0, 512), (subtract_c, 3, 512, 1024), (a_multiply, 8,), (a_quantize, 3, 0,), (a_quantize, 3, 1,), (a_quantize, 3, 2,), (a_multiply, 9,), (subtract_c, 4, 0, 512), (subtract_c, 4, 512, 1024), (subtract_c, 5, 0, 512), (subtract_c, 5, 512, 1024), (a_multiply, 10,), (a_quantize, 4, 0,), (a_quantize, 4, 1,), (a_quantize, 4, 2,), (a_multiply, 11,), (subtract_c, 6, 0, 512), (subtract_c, 6, 512, 1024), (subtract_c, 7, 0, 512), (subtract_c, 7, 512, 1024), (a_quantize, 5, 0,), (a_quantize, 5, 1,), (a_quantize, 5, 2,), (subtract_c, 8, 0, 512), (subtract_c, 8, 512, 1024), (subtract_c, 9, 0, 512), (subtract_c, 9, 512, 1024), (subtract_c, 10, 0, 512), (subtract_c, 10, 512, 1024), (subtract_c, 11, 0, 512), (subtract_c, 11, 512, 768), (subtract_c, 11, 768, 1024)],
-            ))
+            issue([loads, tensor, scalar, vector])

from contextlib import ExitStack

import concourse.mybir as mybir
from concourse.masks import make_identity

M, K, N = 1536, 512, 1024
FLOPS = 2 * M * K * N + 2 * M * M * N + 2 * M * N * N

F32 = mybir.dt.float32
BF16 = mybir.dt.bfloat16
U32 = mybir.dt.uint32
I32 = mybir.dt.int32
U8 = mybir.dt.uint8
FP8 = mybir.dt.float8_e4m3fn
FP8X4 = mybir.dt.float8_e4m3fn_x4
FP4X4 = mybir.dt.float4_e2m1fn_x4
MULT = mybir.AluOpType.mult
SUBTRACT = mybir.AluOpType.subtract

P = 128
PASS = 512
GROUPS = M // PASS
HALVES = N // PASS
BANDS = M // P
LAST = BANDS - 1
PSUM_BANKS = 8

DEPTH = {
    "left_rows": 3,
    "right_rows": 2,
    "field_rows": 4,
    "left_t": 2,
    "right_t": 4,
    "x_t": 4,
    "y_rows": 3,
    "y_t": 2,
    "a_values": 2,
    "a_words": 4,
    "a_t": 4,
    "result": 4,
}


def tile_sylvester_scaled_residual_s8_kernel(
    tc, left, right, a_bytes, a_scale, d, b_words, b_scales, c, out
):
    nc = tc.nc
    with ExitStack() as ctx:
        keep = ctx.enter_context(tc.tile_pool(name="keep", bufs=1))
        work = ctx.enter_context(tc.tile_pool(name="work", bufs=2))
        psum = ctx.enter_context(tc.psum_pool(name="psum", bufs=1))

        ident = keep.tile([P, P], F32, name="ident", align_bytes=64)
        left_codes = keep.tile([P, M], U32, name="left_codes", align_bytes=64)
        left_scales = keep.tile([P, M], U8, name="left_scales", align_bytes=64)
        right_codes = keep.tile([P, N], U32, name="right_codes", align_bytes=64)
        right_scales = keep.tile([P, N], U8, name="right_scales", align_bytes=64)
        x_codes = keep.tile([P, GROUPS, N], U32, name="x_codes", align_bytes=64)
        x_scales = keep.tile([P, GROUPS, N], U8, name="x_scales", align_bytes=64)
        y_codes = keep.tile([P, HALVES, M], U32, name="y_codes", align_bytes=64)
        y_scales = keep.tile([P, HALVES, M], U8, name="y_scales", align_bytes=64)
        a_codes = keep.tile([P, GROUPS, M], U32, name="a_codes", align_bytes=64)
        a_scales = keep.tile([P, GROUPS, M], U8, name="a_scales", align_bytes=64)
        b_codes = keep.tile([P, HALVES, 2 * N], U8, name="b_codes", align_bytes=64)
        b_planes = keep.tile([P, HALVES, N], U8, name="b_planes", align_bytes=64)
        column_scale = keep.tile([P, M], F32, name="column_scale", align_bytes=64)
        code_bytes = [
            keep.tile([P, 4, M], U8, name="code_bytes%d" % g, align_bytes=64) for g in range(GROUPS)
        ]

        held = {}
        free_banks = list(range(PSUM_BANKS))
        bank_number = {}

        def rotating(name, key, shape, dtype):
            if (name, key) not in held:
                new = work.tile(shape, dtype, name=name, bufs=DEPTH[name], align_bytes=64)
                held[name, key] = new
            return held[name, key]

        def take_bank(key):
            number = free_banks.pop(0)
            bank_number[key] = number
            new = psum.tile([P, PASS], F32, name="bank%d" % number, tag="bank%d" % number)
            held["bank", key] = new
            return new

        def give_back(key):
            free_banks.append(bank_number[key])

        def band_rows(src, g):
            return src[PASS * g : PASS * (g + 1), :].rearrange("(p t) n -> p t n", t=4)

        def half(h):
            return slice(PASS * h, PASS * (h + 1))

        def transpose(bank, place, words):
            nc.tensor.transpose(bank[:, P * place : P * (place + 1)], words, ident[:])

        def copy_turned(dst, bank):
            nc.scalar.copy(
                out=dst.rearrange("p c t -> p (c t)").bitcast(F32).rearrange("p (b r u) -> p b r u", b=2, u=2),
                in_=bank[:].rearrange("p (b u r) -> p b r u", b=2, u=2),
            )

        def quantize(codes, planes, values):
            nc.vector.quantize_mx(
                out=codes.bitcast(FP8X4), scales=planes, in_=values.rearrange("p c t -> p (c t)")
            )


        def load_left(g, t0, t1):
            rows = rotating("left_rows", g, [P, 4, K], BF16)
            nc.sync.dma_start(out=rows[:, t0:t1, :], in_=band_rows(left, g)[:, t0:t1, :])

        def load_right(h):
            rows = rotating("right_rows", h, [P, 4, PASS], BF16)
            nc.sync.dma_start(out=rows[:], in_=band_rows(right, 0)[:, :, half(h)])

        def load_d(g, h):
            rows = rotating("field_rows", ("d", g), [P, HALVES, 4, PASS], BF16)
            nc.sync.dma_start(out=rows[:, h], in_=band_rows(d, g)[:, :, half(h)])

        def load_c(g):
            rows = rotating("field_rows", ("c", g), [P, 4, N], BF16)
            nc.sync.dma_start(out=rows[:], in_=band_rows(c, g))

        def load_a(pair):
            g, t = pair // 2, 2 * (pair % 2)
            nc.sync.dma_start(out=code_bytes[g][:, t : t + 2, :], in_=band_rows(a_bytes, g)[:, t : t + 2, :])

        def load_a_scale():
            nc.sync.dma_start(
                out=column_scale[:], in_=a_scale.rearrange("o k -> (o k)").partition_broadcast(P)
            )

        def clear_b_planes():
            nc.vector.memset(b_planes[:].rearrange("p h n -> p (h n)").bitcast(I32), 0)

        def load_b():
            nc.sync.dma_start(out=b_codes[:], in_=b_words.rearrange("h p n -> p h n"))
            for q in range(4):
                nc.sync.dma_start(
                    out=b_planes[32 * q : 32 * q + 4, :, :].bitcast(I32),
                    in_=b_scales[:, 4 * q : 4 * q + 4, :].rearrange("h r n -> r h n").bitcast(I32),
                )

        def store(i, n0, n1):
            nc.sync.dma_start(
                out=band_rows(out, i // 4)[:, i % 4, n0:n1], in_=held["result", i][:, n0:n1]
            )


        def left_turn(g, b2):
            bank = take_bank(("left", g, b2))
            for b in range(2):
                words = held["left_rows", g][:, 2 * b2 + b, :].bitcast(F32)
                for u in range(2):
                    transpose(bank, 2 * b + u, words[:, u : K // 2 : 2])

        def left_out(g, b2):
            key = ("left", g, b2)
            copy_turned(rotating("left_t", (g, b2), [P, 2 * P, 4], BF16)[:], held["bank", key])
            give_back(key)

        def left_quantize(g, b2):
            cols = slice(PASS * g + 2 * P * b2, PASS * g + 2 * P * (b2 + 1))
            quantize(left_codes[:, cols], left_scales[:, cols], held["left_t", (g, b2)][:])


        def right_interleave(h, u):
            copy = nc.scalar.copy if (h, u) == (1, 0) else nc.vector.tensor_copy
            copy(
                out=rotating("right_t", (h, u), [P, PASS // 2, 4], BF16)[:].rearrange("p (q e) t -> p q e t", e=2),
                in_=held["right_rows", h][:].rearrange("p t (q u e) -> p u q e t", u=2, e=2)[:, u],
            )

        def right_quantize(h, u):
            cols = slice(PASS * h + PASS // 2 * u, PASS * h + PASS // 2 * (u + 1))
            quantize(right_codes[:, cols], right_scales[:, cols], held["right_t", (h, u)][:])


        slice_reads = {}

        def slice_read(j, s):
            slice_reads[j, s] = slice_reads.get((j, s), 0) + 1
            if slice_reads[j, s] == 2:
                give_back(("x", j, s))

        def x_matmul(j, s):
            g, h = j // 2, j % 2
            bank = take_bank(("x", j, s))
            cols = slice(PASS * h + P * s, PASS * h + P * (s + 1))
            for t in range(4):
                rows = slice(PASS * g + P * t, PASS * g + P * (t + 1))
                nc.tensor.matmul_mx(
                    out=bank[:, P * t : P * (t + 1)],
                    lhsT=left_codes[:, rows].bitcast(FP8X4),
                    lhsT_scale=left_scales[:, rows],
                    rhs=right_codes[:, cols].bitcast(FP8X4),
                    rhs_scale=right_scales[:, cols],
                    start=True,
                    stop=True,
                )

        def x_out(j, s):
            u, v = s // 2, s % 2
            x_t = rotating("x_t", j, [P, PASS, 4], BF16)
            nc.scalar.copy(
                out=x_t[:].rearrange("p (q u e) t -> p u q e t", u=2, e=2)[:, u, 64 * v : 64 * (v + 1)],
                in_=held["bank", ("x", j, s)][:].rearrange("p (t q e) -> p q e t", t=4, e=2),
            )
            slice_read(j, s)

        def x_quantize(j):
            g, h = j // 2, j % 2
            quantize(x_codes[:, g, half(h)], x_scales[:, g, half(h)], held["x_t", j][:])

        def y_multiply(j, s):
            g, h = j // 2, j % 2
            u, v = s // 2, s % 2
            y_rows = rotating("y_rows", j, [P, 4, 2, PASS // 2], BF16)
            nc.vector.tensor_tensor(
                out=y_rows[:, :, u, P * v : P * (v + 1)].rearrange("p t (q e) -> p t q e", e=2),
                in0=held["bank", ("x", j, s)][:].rearrange("p (t q e) -> p t q e", t=4, e=2),
                in1=held["field_rows", ("d", g)][:, h].rearrange("p t (q u e) -> p u t q e", u=2, e=2)[
                    :, u, :, 64 * v : 64 * (v + 1)
                ],
                op=MULT,
            )
            slice_read(j, s)

        def y_turn(j, b2):
            bank = take_bank(("y", j, b2))
            for b in range(2):
                for u in range(2):
                    transpose(bank, 2 * b + u, held["y_rows", j][:, 2 * b2 + b, u, :].bitcast(F32))

        def y_out(j, b2):
            y_t = rotating("y_t", j, [P, PASS, 4], BF16)
            copy_turned(y_t[:, 2 * P * b2 : 2 * P * (b2 + 1), :], held["bank", ("y", j, b2)])
            give_back(("y", j, b2))

        def y_quantize(j):
            g, h = j // 2, j % 2
            quantize(y_codes[:, h, half(g)], y_scales[:, h, half(g)], held["y_t", j][:])


        def a_multiply(i):
            nc.vector.tensor_tensor(
                out=rotating("a_values", i, [P, M], BF16)[:],
                in0=code_bytes[i // 4][:, i % 4, :].bitcast(FP8),
                in1=column_scale[:],
                op=MULT,
            )

        def a_reorder(i):
            nc.scalar.copy(
                out=rotating("a_words", i, [P, GROUPS, 2, P], F32)[:],
                in_=held["a_values", i][:].bitcast(F32).rearrange("p (g q u) -> p g u q", g=GROUPS, u=2),
            )

        def a_turn(pair, g):
            bank = take_bank(("a", pair, g))
            for b in range(2):
                for u in range(2):
                    transpose(bank, 2 * b + u, held["a_words", 2 * pair + b][:, g, u, :])

        def a_out(pair, g):
            key = ("a", pair, g)
            copy_turned(rotating("a_t", (pair, g), [P, 2 * P, 4], BF16)[:], held["bank", key])
            give_back(key)

        def a_quantize(pair, g):
            cols = slice(2 * P * pair, 2 * P * (pair + 1))
            quantize(a_codes[:, g, cols], a_scales[:, g, cols], held["a_t", (pair, g)][:])


        def multiply_y(i, n0, h, width, **group):
            rows = slice(P * i, P * (i + 1))
            nc.tensor.matmul_mx(
                lhsT=y_codes[:, h, rows].bitcast(FP8X4),
                lhsT_scale=y_scales[:, h, rows],
                rhs=b_codes[:, h, 2 * n0 : 2 * (n0 + width)].bitcast(FP4X4),
                rhs_scale=b_planes[:, h, n0 : n0 + width],
                **group,
            )

        def multiply_a(i, n0, g, width, **group):
            rows = slice(P * i, P * (i + 1))
            nc.tensor.matmul_mx(
                lhsT=a_codes[:, g, rows].bitcast(FP8X4),
                lhsT_scale=a_scales[:, g, rows],
                rhs=x_codes[:, g, n0 : n0 + width].bitcast(FP8X4),
                rhs_scale=x_scales[:, g, n0 : n0 + width],
                **group,
            )

        passes_done = {}

        def next_pass(i, n0):
            count = passes_done.get((i, n0), 0) + 1
            passes_done[i, n0] = count
            if count == 1:
                take_bank(("out", i, n0))
            return dict(
                width=PASS,
                out=held["bank", ("out", i, n0)][:],
                start=(count == 1),
                stop=(count == HALVES + GROUPS),
            )

        def y_pass(i, n0, h):
            multiply_y(i, n0, h, **next_pass(i, n0))

        def a_pass(i, n0, g):
            multiply_a(i, n0, g, **next_pass(i, n0))

        def narrow_sum(i, n0):
            bank0 = n0 - n0 % (2 * P)
            if n0 == bank0:
                take_bank(("out", i, bank0))
            piece = held["bank", ("out", i, bank0)][:, n0 - bank0 : n0 - bank0 + P]
            for h in range(HALVES):
                multiply_y(i, n0, h, width=P, out=piece, start=(h == 0), stop=False)
            for g in range(GROUPS):
                multiply_a(i, n0, g, width=P, out=piece, start=False, stop=(g == GROUPS - 1))

        def subtract_c(i, n0, n1):
            nc.vector.tensor_tensor(
                out=rotating("result", i, [P, N], F32)[:, n0:n1],
                in0=held["bank", ("out", i, n0)][:, : n1 - n0],
                in1=held["field_rows", ("c", i // 4)][:, i % 4, n0:n1],
                op=SUBTRACT,
            )
            give_back(("out", i, n0))


        def both(f, *x):
            return [(f, *x, 0), (f, *x, 1)]

        def freed(name, n, last_reads):
            return last_reads(n - DEPTH[name]) if n >= DEPTH[name] else []

        def slices(f, j):
            return [(f, j, s) for s in range(4)]

        def sums(i, n0, n1):
            if n1 - n0 < PASS:
                return [(narrow_sum, i, n0), (narrow_sum, i, n0 + P)]
            return [(y_pass, i, n0, h) for h in range(HALVES)] + [(a_pass, i, n0, g) for g in range(GROUPS)]

        after = {
            left_turn: lambda g, b2: [(load_left, g, 2 * b2, 2 * b2 + 2) if g == 0 else (load_left, g, 0, 4)],
            left_out: lambda g, b2: [(left_turn, g, b2)]
            + freed("left_t", 2 * g + b2, lambda n: [(left_quantize, n // 2, n % 2)]),
            left_quantize: lambda g, b2: [(left_out, g, b2)],
            right_interleave: lambda h, u: [(load_right, h)],
            right_quantize: lambda h, u: [(right_interleave, h, u)],
            x_matmul: lambda j, s: both(left_quantize, j // 2) + [(right_quantize, j % 2, s // 2)],
            x_out: lambda j, s: [(x_matmul, j, s)] + freed("x_t", j, lambda n: [(x_quantize, n)]),
            x_quantize: lambda j: slices(x_out, j),
            y_multiply: lambda j, s: [(x_matmul, j, s), (load_d, j // 2, j % 2)]
            + freed("y_rows", j, lambda n: both(y_turn, n)),
            y_turn: lambda j, b2: slices(y_multiply, j),
            y_out: lambda j, b2: [(y_turn, j, b2)] + freed("y_t", j, lambda n: [(y_quantize, n)]),
            y_quantize: lambda j: both(y_out, j),
            a_multiply: lambda i: [(load_a_scale,), (load_a, i // 2)]
            + freed("a_values", i, lambda n: [(a_reorder, n)]),
            a_reorder: lambda i: [(a_multiply, i)]
            + freed("a_words", i, lambda n: [(a_turn, n // 2, g) for g in range(GROUPS)]),
            a_turn: lambda pair, g: both_bands(a_reorder, pair),
            a_out: lambda pair, g: [(a_turn, pair, g)]
            + freed("a_t", GROUPS * pair + g, lambda n: [(a_quantize, n // GROUPS, n % GROUPS)]),
            a_quantize: lambda pair, g: [(a_out, pair, g)],
            y_pass: lambda i, n0, h: [(load_b,), (y_quantize, 2 * (i // 4) + h)],
            a_pass: lambda i, n0, g: [(a_quantize, i // 2, g), (x_quantize, 2 * g + n0 // PASS)],
            narrow_sum: lambda i, n0: [(load_b,)]
            + [(y_quantize, 2 * (i // 4) + h) for h in range(HALVES)]
            + [(a_quantize, i // 2, g) for g in range(GROUPS)]
            + [(x_quantize, 2 * g + n0 // PASS) for g in range(GROUPS)],
            subtract_c: lambda i, n0, n1: sums(i, n0, n1)
            + [(load_c, i // 4)]
            + freed("result", i, lambda n: [(store, n, 0, N)]),
            store: lambda i, n0, n1: both_halves(i) if n1 - n0 == N else [(subtract_c, i, n0, n1)],
            load_b: lambda: [(clear_b_planes,)],
            load_c: lambda g: freed("field_rows", GROUPS + g, lambda n: slices(y_multiply, 2 * n) + slices(y_multiply, 2 * n + 1)),
        }

        def both_bands(f, pair):
            return [(f, 2 * pair), (f, 2 * pair + 1)]

        def both_halves(i):
            return [(subtract_c, i, PASS * n, PASS * (n + 1)) for n in range(HALVES)]

        def opens_bank(f, x):
            if f in (y_pass, a_pass):
                return x[:2] not in passes_done
            if f == narrow_sum:
                return x[1] % (2 * P) == 0
            return f in (left_turn, x_matmul, y_turn, a_turn)

        def issue(queues):
            waiting = [list(q) for q in queues]
            issued = set()
            while any(waiting):
                before = len(issued)
                for q in waiting:
                    if not q:
                        continue
                    f, x = q[0][0], q[0][1:]
                    ready = all(s in issued for s in (after[f](*x) if f in after else []))
                    if ready and (free_banks or not opens_bank(f, x)):
                        f(*x)
                        issued.add(q.pop(0))
                assert len(issued) > before


        def units(f, pair):
            return [(f, pair, g) for g in range(GROUPS)]

        def y_passes(i):
            return [(y_pass, i, PASS * n, h) for h in range(HALVES) for n in range(HALVES)]

        def a_passes(i, *groups):
            return [(a_pass, i, PASS * n, g) for g in groups for n in range(HALVES)]

        def some(f, j, *picked):
            return [(f, j, s) for s in picked]

        pairs = BANDS // 2
        loads = [(load_left, 0, 0, 2), (load_left, 0, 2, 4), (load_right, 0), (load_right, 1)]
        loads += [(load_left, 1, 0, 4), (load_d, 0, 0), (load_a, 0), (load_d, 0, 1), (load_left, 2, 0, 4)]
        loads += [(load_a_scale,)] + both(load_d, 1) + [(load_a, 1), (load_b,), (load_a, 2)] + both(load_d, 2)
        loads += [(load_c, 0), (load_c, 1), (load_a, 3), (load_a, 4), (load_c, 2), (load_a, 5)]
        loads += [(store, i, 0, N) for i in range(LAST)]
        loads += [(store, LAST, 0, PASS), (store, LAST, PASS, PASS + 2 * P), (store, LAST, PASS + 2 * P, N)]

        tensor = both(left_turn, 0) + some(x_matmul, 0, 0, 1) + both(left_turn, 1)
        tensor += slices(x_matmul, 1) + some(x_matmul, 0, 2, 3) + both(left_turn, 2) + both(y_turn, 0)
        tensor += slices(x_matmul, 2) + slices(x_matmul, 3) + both(y_turn, 1)
        tensor += some(x_matmul, 4, 0, 1) + units(a_turn, 0) + some(x_matmul, 4, 2, 3) + both(y_turn, 2)
        tensor += some(x_matmul, 5, 0, 1) + y_passes(0) + some(x_matmul, 5, 2, 3)
        tensor += a_passes(0, 0, 1) + y_passes(1) + a_passes(1, 0) + units(a_turn, 1) + a_passes(1, 1)
        tensor += both(y_turn, 3) + both(y_turn, 4) + a_passes(0, 2) + y_passes(2) + a_passes(1, 2)
        tensor += a_passes(2, 0, 1, 2) + both(y_turn, 5) + units(a_turn, 2) + y_passes(3) + a_passes(3, 0, 1, 2)
        for pair in range(2, pairs - 1):
            tensor += y_passes(2 * pair) + a_passes(2 * pair, 0, 1, 2)
            tensor += y_passes(2 * pair + 1) + a_passes(2 * pair + 1, 0)
            tensor += units(a_turn, pair + 1) + a_passes(2 * pair + 1, 1, 2)
        tensor += y_passes(LAST - 1) + a_passes(LAST - 1, 0, 1, 2)
        tensor += sums(LAST, 0, PASS) + [(narrow_sum, LAST, n0) for n0 in range(PASS, N, P)]

        scalar = both(left_out, 0) + [(right_interleave, 1, 0)] + some(x_out, 0, 0, 1) + both(left_out, 1)
        scalar += some(x_out, 0, 2, 3) + some(x_out, 1, 0) + both(left_out, 2) + some(x_out, 1, 1, 2, 3)
        scalar += both(y_out, 0) + slices(x_out, 2) + [(a_reorder, 0)] + some(x_out, 3, 0, 1, 2)
        scalar += both(y_out, 1) + [(a_reorder, 1)] + some(x_out, 3, 3) + some(x_out, 4, 0, 1)
        scalar += units(a_out, 0) + some(x_out, 4, 2, 3) + [(a_reorder, 2)] + both(y_out, 2)
        scalar += slices(x_out, 5) + [(a_reorder, 3)] + units(a_out, 1) + both(y_out, 3) + both(y_out, 4)
        scalar += both_bands(a_reorder, 2) + units(a_out, 2) + both(y_out, 5)
        for pair in range(3, pairs):
            scalar += both_bands(a_reorder, pair) + units(a_out, pair)

        vector = [(clear_b_planes,), (right_interleave, 0, 0)] + both(left_quantize, 0) + [(right_quantize, 0, 0)]
        vector += [(right_interleave, 0, 1), (right_interleave, 1, 1)]
        vector += [(right_quantize, 0, 1), (right_quantize, 1, 1), (right_quantize, 1, 0)]
        vector += some(y_multiply, 0, 0, 1) + some(y_multiply, 1, 0) + both(left_quantize, 1)
        vector += some(y_multiply, 1, 1, 2, 3) + some(y_multiply, 0, 2, 3) + both(left_quantize, 2)
        vector += [(x_quantize, 0), (a_multiply, 0)] + some(y_multiply, 2, 0) + [(x_quantize, 1)]
        vector += some(y_multiply, 2, 1, 2) + [(y_quantize, 0), (a_multiply, 1)] + some(y_multiply, 2, 3)
        vector += some(y_multiply, 3, 0, 1, 3, 2) + [(a_multiply, 2), (x_quantize, 2)]
        vector += some(y_multiply, 4, 0, 1) + [(x_quantize, 3), (y_quantize, 1)] + units(a_quantize, 0)
        vector += some(y_multiply, 4, 2, 3) + [(a_multiply, 3)] + slices(y_multiply, 5)
        vector += [(x_quantize, 4), (x_quantize, 5)] + units(a_quantize, 1) + [(y_quantize, 2)]
        vector += both_bands(a_multiply, 2) + both_halves(0) + both_halves(1) + [(y_quantize, 3), (a_multiply, 6)]
        vector += units(a_quantize, 2) + both_halves(2) + [(y_quantize, 4), (a_multiply, 7), (y_quantize, 5)]
        vector += both_halves(3)
        for pair in range(4, pairs):
            vector += [(a_multiply, 2 * pair)] + units(a_quantize, pair - 1) + [(a_multiply, 2 * pair + 1)]
            vector += both_halves(2 * pair - 4) + both_halves(2 * pair - 3)
        vector += units(a_quantize, pairs - 1)
        for i in range(2 * pairs - 4, LAST):
            vector += both_halves(i)
        vector += [(subtract_c, LAST, 0, PASS)]
        vector += [(subtract_c, LAST, n0, n0 + 2 * P) for n0 in range(PASS, N, 2 * P)]

        make_identity(nc, ident[:])
        with tc.manual_schedule():
            issue([loads, tensor, scalar, vector])
